import numpy as np
import ml_dtypes


def mxq(x, axis, fmt="e4m3"):
    dtype, down = {"e4m3": (ml_dtypes.float8_e4m3fn, 7), "e5m2": (ml_dtypes.float8_e5m2, 14)}[fmt]
    v = np.moveaxis(np.asarray(x, np.float32).astype(ml_dtypes.bfloat16).astype(np.float64), axis, -1)
    blocks = v.reshape(v.shape[:-1] + (-1, 32))
    amax = np.abs(blocks).max(-1, keepdims=True)
    byte = np.maximum(np.where(amax > 0, np.frexp(amax)[1] - 1 + 127, 0) - down, 1)
    scale = np.exp2(byte - 127.0)
    codes = (blocks / scale).astype(np.float32).astype(dtype).astype(np.float64)
    return np.moveaxis((codes * scale).reshape(v.shape), -1, axis)


WIDE = False


def mx_kscale(k):
    if not WIDE:
        return np.ones(k)
    levels = np.array([10, -10, 5, -5, 0])
    if k % 512:
        return np.exp2(np.random.permutation(np.resize(levels, k // 32))).repeat(32)
    a = np.empty((k // 512, 16))
    for p in range(k // 512):
        a[p, :8] = np.random.permutation(np.resize(levels, 8))
        for g in range(8):
            far = levels[np.abs(levels - a[p, g]) >= 10]
            a[p, g + 8] = far[np.random.randint(len(far))]
    return np.exp2(a.ravel()).repeat(32)


def f64(x):
    return np.asarray(x).astype(np.float64)


def striped(idx):
    return np.tile(idx.reshape(-1, 16).T, (8, 1)).astype(np.uint16)


def unstriped(offs):
    return offs[:16].T.reshape(-1).astype(np.int64)


E2M1 = np.array([0.0, 0.5, 1.0, 1.5, 2.0, 3.0, 4.0, 6.0, -0.0, -0.5, -1.0, -1.5, -2.0, -3.0, -4.0, -6.0])


def pack_weight(w, fmt):
    k, n = w.shape
    w = f64(np.asarray(w, np.float32).astype(ml_dtypes.bfloat16)).reshape(k // 32, 32, n)
    amax = np.abs(w).max(1)
    if fmt == "e4m3":
        byte = np.frexp(amax)[1] - 1 + 127 - 7
    else:
        mant, ex = np.frexp(amax / 6.0)
        byte = np.where(mant > 0.5, ex, ex - 1) + 127
    byte = np.clip(np.where(amax > 0, byte, 1), 1, 254)
    scaled = (w * np.exp2(127.0 - byte)[:, None, :]).reshape(k, n).astype(np.float32)
    by_word = np.ascontiguousarray(scaled.reshape(k // 512, 128, 4, n).transpose(0, 1, 3, 2))
    if fmt == "e4m3":
        words = by_word.astype(ml_dtypes.float8_e4m3fn).view(np.uint8)
    else:
        c = by_word.astype(ml_dtypes.float4_e2m1fn).view(np.uint8) & 0xF
        words = (c[..., 0::2] | (c[..., 1::2] << 4)).reshape(k // 512, 128, 2 * n)
    return np.ascontiguousarray(words), np.ascontiguousarray(byte.astype(np.uint8).reshape(k // 512, 16, n))


def unpack_weight(words, scales, fmt):
    g, _, n = scales.shape
    words = np.ascontiguousarray(words).reshape(g, 128, n, -1)
    if fmt == "e4m3":
        vals = words.view(ml_dtypes.float8_e4m3fn).astype(np.float64)
    else:
        nib = np.empty((g, 128, n, 4), np.uint8)
        nib[..., 0::2] = words & 0xF
        nib[..., 1::2] = words >> 4
        vals = E2M1[nib]
    vals = vals * np.repeat(np.exp2(scales.astype(np.float64) - 127.0), 8, axis=1)[..., None]
    return vals.transpose(0, 1, 3, 2).reshape(g * 512, n)


def pack_table(v):
    words, scales = pack_weight(v, "e4m3")
    return np.concatenate([words.reshape(words.shape[0], -1), scales.reshape(scales.shape[0], -1)], axis=1)


def unpack_table(tab):
    g, t = tab.shape[0], tab.shape[1] // 528
    return unpack_weight(tab[:, :512 * t].reshape(g, 128, t, 4), tab[:, 512 * t:].reshape(g, 16, t), "e4m3")


K, H, M, T, S = 1024, 1536, 512, 512, 256


def setup_inputs():
    n = np.random.standard_normal
    s = mx_kscale(K)[:, None]
    u = mx_kscale(H)[:, None]
    w2 = 1.4 * n((H, M)) / np.sqrt(H) / u
    p_w8 = pack_weight(w2[:512], "e4m3")
    p_w4 = pack_weight(w2[512:], "e2m1")
    return {
        "tab": pack_table(n((K, T)) * s),
        "w1": (n((K, H)) / np.sqrt(K) / s * u.T).astype(np.float32),
        "w8_words": p_w8[0],
        "w8_scales": p_w8[1],
        "w4_words": p_w4[0],
        "w4_scales": p_w4[1],
        "prev": (n((512, 256))).astype(np.float32),
        "offs": striped(np.random.permutation(T)[:S]),
    }


def reference(tab, w1, w8_words, w8_scales, w4_words, w4_scales, prev, offs):
    tab_ = unpack_table(tab)[:, unstriped(offs)]
    w1_ = mxq(f64(w1), 0, "e4m3")
    w8_ = unpack_weight(w8_words, w8_scales, "e4m3")
    w4_ = unpack_weight(w4_words, w4_scales, "e2m1")
    h_ = mxq(np.maximum(w1_.T @ tab_, 0.0), 0, "e4m3")
    y = w8_.T @ h_[:512] + w4_.T @ h_[512:]
    return f64(prev) + y

@@ -1,0 +1,232 @@
+from contextlib import ExitStack
+
+import concourse.mybir as mybir
+
+FLOPS = 1207959552
+
+P = 128
+K, H, M, T, S = 1024, 1536, 512, 512, 256
+HALF = 128
+WORD_BYTES = 512 * T
+
+F32 = mybir.dt.float32
+BF16 = mybir.dt.bfloat16
+I32 = mybir.dt.int32
+U32 = mybir.dt.uint32
+U16 = mybir.dt.uint16
+U8 = mybir.dt.uint8
+FP8 = mybir.dt.float8_e4m3fn_x4
+FP4 = mybir.dt.float4_e2m1fn_x4
+RELU = mybir.ActivationFunctionType.Relu
+
+
+def tile_list_tabmlp_mix_res_kernel(
+    tc, tab, w1, w8_words, w8_scales, w4_words, w4_scales, prev, offs, out
+):
+    nc = tc.nc
+    with ExitStack() as ctx:
+        keep = ctx.enter_context(tc.tile_pool(name="keep", bufs=1))
+        psum = ctx.enter_context(tc.psum_pool(name="psum", bufs=1))
+
+        offsets = keep.tile([P, S // 16], U16, name="offsets")
+        table_words = [keep.tile([P, T], I32, name=f"table_words{a}", align_bytes=64) for a in range(2)]
+        table_scales = keep.tile([P, T // 4], I32, name="table_scales", align_bytes=64)
+        w2_scales = keep.tile([P, 3, M // 4], I32, name="w2_scales", align_bytes=64)
+        w8_codes = keep.tile([P, M], I32, name="w8_codes", align_bytes=64)
+        w4_codes = keep.tile([P, 2, M // 2], I32, name="w4_codes", align_bytes=64)
+        prev_sb = keep.tile([P, 4, S], F32, name="prev_sb")
+
+        nc.vector.memset(table_scales[:], 0)
+        nc.vector.memset(w2_scales[:], 0)
+
+        raws = {}
+
+        def load_w1(a, b, c0, c1):
+            raw = keep.tile([P, 4, c1 - c0], F32, name=f"raw{a}{b}_{c0}", align_bytes=64)
+            rows = w1[512 * a : 512 * (a + 1), 512 * b + c0 : 512 * b + c1]
+            nc.sync.dma_start(raw[:], rows.rearrange("(p j) c -> p j c", j=4))
+            raws.setdefault((b, a), []).append((c0, c1, raw))
+
+        tab_i32 = tab.bitcast(I32)
+        tab_scale_rows = tab_i32[:, WORD_BYTES // 4 :].rearrange("a (q c) -> a q c", q=16)
+        w8_rows = w8_scales.bitcast(I32)
+        w4_rows = w4_scales.bitcast(I32)
+
+        def load_w8_scales(q):
+            nc.gpsimd.dma_start(w2_scales[32 * q : 32 * q + 4, 0, :], w8_rows[0, 4 * q : 4 * q + 4, :])
+
+        def load_w4_scales(q):
+            nc.gpsimd.dma_start(
+                w2_scales[32 * q : 32 * q + 4, 1:3, :], w4_rows[:, 4 * q : 4 * q + 4, :].rearrange("a q c -> q a c")
+            )
+
+        for a in range(2):
+            nc.sync.dma_start(
+                table_words[a][:], tab_i32[a, 0 : WORD_BYTES // 4].rearrange("(p c) -> p c", p=P)
+            )
+        nc.sync.dma_start(offsets[:], offs)
+        load_w1(0, 0, 0, 512)
+        for q in range(4):
+            nc.sync.dma_start(table_scales[32 * q : 32 * q + 8, :], tab_scale_rows[:, 4 * q : 4 * q + 4, :])
+        for q in range(4):
+            load_w8_scales(q)
+        for q in range(4):
+            load_w4_scales(q)
+        load_w1(1, 0, 0, 512)
+        load_w1(0, 1, 0, 512)
+        load_w1(1, 1, 0, 512)
+        load_w1(0, 2, 0, 512)
+        load_w1(1, 2, 0, 384)
+        load_w1(1, 2, 384, 512)
+        nc.sync.dma_start(w8_codes[:], w8_words[0].rearrange("p n i -> p (n i)").bitcast(I32))
+        nc.sync.dma_start(w4_codes[:], w4_words.bitcast(I32).rearrange("a p c -> p a c"))
+        nc.sync.dma_start(prev_sb[:], prev.rearrange("(m p) j -> p m j", p=P))
+
+        picked_words = []
+        for a in range(2):
+            words = keep.tile([P, S], U32, name=f"picked_words{a}", align_bytes=64)
+            nc.vector.tensor_copy(words[:], table_words[a][:].bitcast(U32).indirect(offsets[:]))
+            picked_words.append(words)
+        picked_scales = keep.tile([P, S], U8, name="picked_scales", align_bytes=64)
+        nc.vector.tensor_copy(picked_scales[:], table_scales[:].bitcast(U8).indirect(offsets[:]))
+
+        grouped, codes, scales = {}, {}, {}
+        for b in range(3):
+            for a in range(2):
+                grouped[b, a] = keep.tile([P, 2048], BF16, name=f"grouped{b}{a}", align_bytes=64)
+                codes[b, a] = keep.tile([P, 512], U32, name=f"w1_codes{b}{a}", align_bytes=64)
+                scales[b, a] = keep.tile([P, 512], U8, name=f"w1_scales{b}{a}", align_bytes=64)
+
+        def interleave(b, a):
+            view = grouped[b, a][:].rearrange("p (t m j) -> p m j t", t=4, j=4)
+            for c0, c1, raw in raws[b, a]:
+                src = raw[:].rearrange("p j (m t) -> p m j t", t=4)
+                m0, n = c0 // 4, (c1 - c0) // 4
+                cut = {128: 76, 96: 48, 32: 32}[n]
+                if cut < n:
+                    nc.scalar.copy(view[:, m0 + cut : m0 + n], src[:, cut:n])
+                nc.vector.tensor_copy(view[:, m0 : m0 + cut], src[:, 0:cut])
+
+        def quantise(b, a, step):
+            for i in range(0, 2048, step):
+                o = slice(i // 4, (i + step) // 4)
+                nc.vector.quantize_mx(
+                    out=codes[b, a][:, o].bitcast(FP8),
+                    scales=scales[b, a][:, o],
+                    in_=grouped[b, a][:, i : i + step],
+                )
+
+        def hidden_matmuls(b):
+            banks = [psum.tile([P, 4, HALF], F32, name=f"hidden{b % 2}{h}") for h in range(2)]
+            for t in range(4):
+                cols = slice(HALF * t, HALF * (t + 1))
+                for a in range(2):
+                    for h in range(2):
+                        toks = slice(HALF * h, HALF * (h + 1))
+                        nc.tensor.matmul_mx(
+                            out=banks[h][:, t, :],
+                            lhsT=codes[b, a][:, cols].bitcast(FP8),
+                            lhsT_scale=scales[b, a][:, cols],
+                            rhs=picked_words[a][:, toks].bitcast(FP8),
+                            rhs_scale=picked_scales[4 * a : P, toks],
+                            start=a == 0,
+                            stop=a == 1,
+                        )
+            return banks
+
+        h_grouped, h_codes, h_scales = {}, {}, {}
+        shared = {(1, 0): "raw12_384", (1, 1): "raw12_0"}
+        for b in range(3):
+            h_scales[b] = keep.tile([P, S], U8, name=f"h_scales{b}", align_bytes=64)
+
+        def relu(engine, b, h, bank):
+            name = shared.get((b, h), f"h_grouped{b}{h}")
+            tile = keep.tile([P, HALF, 4], BF16, name=name, align_bytes=64)
+            src = bank[:].rearrange("p t n -> p n t")
+            if engine is nc.scalar:
+                nc.scalar.activation(tile[:], src, RELU)
+            else:
+                nc.vector.tensor_scalar_max(tile[:], src, 0.0)
+            h_grouped[b, h] = tile
+
+        def hidden_quantise(b):
+            h_codes[b] = keep.tile([P, S], U32, name="grouped21" if b == 1 else f"h_codes{b}", align_bytes=64)
+            for h in range(2):
+                toks = slice(HALF * h, HALF * (h + 1))
+                nc.vector.quantize_mx(
+                    out=h_codes[b][:, toks].bitcast(FP8),
+                    scales=h_scales[b][:, toks],
+                    in_=h_grouped[b, h][:].rearrange("p n t -> p (n t)"),
+                )
+
+        def out_matmul(acc, m, h, b):
+            if b == 0:
+                lhsT = w8_codes[:, HALF * m : HALF * (m + 1)].bitcast(FP8)
+            else:
+                lhsT = w4_codes[:, b - 1, 64 * m : 64 * (m + 1)].bitcast(FP4)
+            nc.tensor.matmul_mx(
+                out=acc[:],
+                lhsT=lhsT,
+                lhsT_scale=w2_scales[:, b, 32 * m : 32 * (m + 1)].bitcast(U8),
+                rhs=h_codes[b][:, HALF * h : HALF * (h + 1)].bitcast(FP8),
+                rhs_scale=h_scales[b][:, HALF * h : HALF * (h + 1)],
+                start=b == 0,
+                stop=b == 2,
+            )
+
+        acc = {}
+
+        def start_out(m, h, name):
+            acc[m, h] = psum.tile([P, HALF], F32, name=name)
+            out_matmul(acc[m, h], m, h, 0)
+
+        def finish_out(m):
+            res = keep.tile([P, S], F32, name=f"res{m}")
+            for h in range(2):
+                out_matmul(acc[m, h], m, h, 2)
+                toks = slice(HALF * h, HALF * (h + 1))
+                nc.vector.tensor_add(res[:, toks], acc[m, h][:], prev_sb[:, m, toks])
+                if m == 3:
+                    queue = nc.scalar if h == 0 else nc.sync
+                    queue.dma_start(out[P * m : P * (m + 1), toks], res[:, toks])
+            if m < 3:
+                queue = nc.scalar if m == 1 else nc.sync
+                queue.dma_start(out[P * m : P * (m + 1), :], res[:])
+
+        interleave(0, 0)
+        quantise(0, 0, 1024)
+        interleave(0, 1)
+        quantise(0, 1, 1024)
+        banks = hidden_matmuls(0)
+        interleave(1, 0)
+        quantise(1, 0, 1024)
+        interleave(1, 1)
+        relu(nc.scalar, 0, 0, banks[0])
+        relu(nc.vector, 0, 1, banks[1])
+        quantise(1, 1, 1024)
+        banks = hidden_matmuls(1)
+        hidden_quantise(0)
+        interleave(2, 0)
+        quantise(2, 0, 1024)
+        interleave(2, 1)
+        quantise(2, 1, 512)
+        relu(nc.scalar, 1, 0, banks[0])
+        relu(nc.scalar, 1, 1, banks[1])
+        hidden_quantise(1)
+        banks = hidden_matmuls(2)
+        for m in range(2):
+            for h in range(2):
+                start_out(m, h, f"acc{m}{h}")
+        for h in range(2):
+            start_out(2, h, f"hidden1{h}")
+        for m in range(3):
+            for h in range(2):
+                out_matmul(acc[m, h], m, h, 1)
+        relu(nc.scalar, 2, 0, banks[0])
+        relu(nc.vector, 2, 1, banks[1])
+        for h in range(2):
+            start_out(3, h, f"hidden0{h}")
+            out_matmul(acc[3, h], 3, h, 1)
+        hidden_quantise(2)
+        for m in range(4):
+            finish_out(m)

@@ -40,46 +40,42 @@ def tile_list_tabmlp_mix_res_kernel(
         nc.vector.memset(w2_scales[:], 0)
 
         raws = {}
+        first, second, last = 1, 2, 0
 
-        def load_w1(a, b, c0, c1):
-            raw = keep.tile([P, 4, c1 - c0], F32, name=f"raw{a}{b}_{c0}", align_bytes=64)
+        def load_w1(b, a, c0, c1):
+            raw = keep.tile([P, 4, c1 - c0], F32, name=f"raw{b}{a}_{c0}", align_bytes=64)
             rows = w1[512 * a : 512 * (a + 1), 512 * b + c0 : 512 * b + c1]
             nc.sync.dma_start(raw[:], rows.rearrange("(p j) c -> p j c", j=4))
-            raws.setdefault((b, a), []).append((c0, c1, raw))
+            raws[b, a, c0] = raw
 
         tab_i32 = tab.bitcast(I32)
         tab_scale_rows = tab_i32[:, WORD_BYTES // 4 :].rearrange("a (q c) -> a q c", q=16)
         w8_rows = w8_scales.bitcast(I32)
         w4_rows = w4_scales.bitcast(I32)
 
-        def load_w8_scales(q):
-            nc.gpsimd.dma_start(w2_scales[32 * q : 32 * q + 4, 0, :], w8_rows[0, 4 * q : 4 * q + 4, :])
-
-        def load_w4_scales(q):
-            nc.gpsimd.dma_start(
-                w2_scales[32 * q : 32 * q + 4, 1:3, :], w4_rows[:, 4 * q : 4 * q + 4, :].rearrange("a q c -> q a c")
-            )
-
         for a in range(2):
             nc.sync.dma_start(
                 table_words[a][:], tab_i32[a, 0 : WORD_BYTES // 4].rearrange("(p c) -> p c", p=P)
             )
         nc.sync.dma_start(offsets[:], offs)
-        load_w1(0, 0, 0, 512)
         for q in range(4):
             nc.sync.dma_start(table_scales[32 * q : 32 * q + 8, :], tab_scale_rows[:, 4 * q : 4 * q + 4, :])
+        load_w1(first, 0, 0, 512)
+        load_w1(first, 1, 0, 512)
         for q in range(4):
-            load_w8_scales(q)
+            nc.sync.dma_start(
+                w2_scales[32 * q : 32 * q + 4, 1:3, :], w4_rows[:, 4 * q : 4 * q + 4, :].rearrange("a q c -> q a c")
+            )
+        load_w1(second, 0, 0, 512)
         for q in range(4):
-            load_w4_scales(q)
-        load_w1(1, 0, 0, 512)
-        load_w1(0, 1, 0, 512)
-        load_w1(1, 1, 0, 512)
-        load_w1(0, 2, 0, 512)
-        load_w1(1, 2, 0, 384)
-        load_w1(1, 2, 384, 512)
-        nc.sync.dma_start(w8_codes[:], w8_words[0].rearrange("p n i -> p (n i)").bitcast(I32))
+            nc.sync.dma_start(w2_scales[32 * q : 32 * q + 4, 0, :], w8_rows[0, 4 * q : 4 * q + 4, :])
+        load_w1(second, 1, 0, 512)
+        load_w1(last, 0, 0, 512)
+        load_w1(last, 1, 0, 256)
+        load_w1(last, 1, 256, 384)
+        load_w1(last, 1, 384, 512)
         nc.sync.dma_start(w4_codes[:], w4_words.bitcast(I32).rearrange("a p c -> p a c"))
+        nc.sync.dma_start(w8_codes[:], w8_words[0].rearrange("p n i -> p (n i)").bitcast(I32))
         nc.sync.dma_start(prev_sb[:], prev.rearrange("(m p) j -> p m j", p=P))
 
         picked_words = []
@@ -93,140 +89,144 @@ def tile_list_tabmlp_mix_res_kernel(
         grouped, codes, scales = {}, {}, {}
         for b in range(3):
             for a in range(2):
-                grouped[b, a] = keep.tile([P, 2048], BF16, name=f"grouped{b}{a}", align_bytes=64)
+                for u in range(2):
+                    grouped[b, a, u] = keep.tile([P, 1024], BF16, name=f"grouped{b}{a}{u}", align_bytes=64)
                 codes[b, a] = keep.tile([P, 512], U32, name=f"w1_codes{b}{a}", align_bytes=64)
                 scales[b, a] = keep.tile([P, 512], U8, name=f"w1_scales{b}{a}", align_bytes=64)
 
-        def interleave(b, a):
-            view = grouped[b, a][:].rearrange("p (t m j) -> p m j t", t=4, j=4)
-            for c0, c1, raw in raws[b, a]:
-                src = raw[:].rearrange("p j (m t) -> p m j t", t=4)
-                m0, n = c0 // 4, (c1 - c0) // 4
-                cut = {128: 76, 96: 48, 32: 32}[n]
-                if cut < n:
-                    nc.scalar.copy(view[:, m0 + cut : m0 + n], src[:, cut:n])
-                nc.vector.tensor_copy(view[:, m0 : m0 + cut], src[:, 0:cut])
+        def interleave(engine, b, a, c0, u, m0, m1):
+            view = grouped[b, a, u][:].rearrange("p (t m j) -> p m j t", t=2, j=4)
+            src = raws[b, a, c0][:].rearrange("p j (m t) -> p m j t", t=4)
+            dst = view[:, m0:m1]
+            src = src[:, m0 - c0 // 4 : m1 - c0 // 4, :, 2 * u : 2 * u + 2]
+            if engine is nc.scalar:
+                nc.scalar.copy(dst, src)
+            else:
+                nc.vector.tensor_copy(dst, src)
 
-        def quantise(b, a, step):
-            for i in range(0, 2048, step):
-                o = slice(i // 4, (i + step) // 4)
-                nc.vector.quantize_mx(
-                    out=codes[b, a][:, o].bitcast(FP8),
-                    scales=scales[b, a][:, o],
-                    in_=grouped[b, a][:, i : i + step],
-                )
+        def quantise(b, a, u, i0, i1):
+            o = slice(256 * u + i0 // 4, 256 * u + i1 // 4)
+            nc.vector.quantize_mx(
+                out=codes[b, a][:, o].bitcast(FP8), scales=scales[b, a][:, o], in_=grouped[b, a, u][:, i0:i1]
+            )
 
-        def hidden_matmuls(b):
-            banks = [psum.tile([P, 4, HALF], F32, name=f"hidden{b % 2}{h}") for h in range(2)]
-            for t in range(4):
+        def whole_block(b, a):
+            interleave(nc.scalar, b, a, 0, 1, 0, 128)
+            interleave(nc.vector, b, a, 0, 0, 0, 128)
+            quantise(b, a, 0, 0, 1024)
+            quantise(b, a, 1, 0, 1024)
+
+        banks = {}
+
+        def hidden_matmuls(b, steps):
+            for h in range(2):
+                banks[b, h] = psum.tile([P, 4, HALF], F32, name=f"hidden{int(b == second)}{h}")
+            for a, t in steps:
                 cols = slice(HALF * t, HALF * (t + 1))
-                for a in range(2):
-                    for h in range(2):
-                        toks = slice(HALF * h, HALF * (h + 1))
-                        nc.tensor.matmul_mx(
-                            out=banks[h][:, t, :],
-                            lhsT=codes[b, a][:, cols].bitcast(FP8),
-                            lhsT_scale=scales[b, a][:, cols],
-                            rhs=picked_words[a][:, toks].bitcast(FP8),
-                            rhs_scale=picked_scales[4 * a : P, toks],
-                            start=a == 0,
-                            stop=a == 1,
-                        )
-            return banks
+                for h in range(2):
+                    toks = slice(HALF * h, HALF * (h + 1))
+                    nc.tensor.matmul_mx(
+                        out=banks[b, h][:, t, :],
+                        lhsT=codes[b, a][:, cols].bitcast(FP8),
+                        lhsT_scale=scales[b, a][:, cols],
+                        rhs=picked_words[a][:, toks].bitcast(FP8),
+                        rhs_scale=picked_scales[4 * a : P, toks],
+                        start=(a, t) == steps[0],
+                        stop=(a, t) == steps[-1],
+                    )
 
         h_grouped, h_codes, h_scales = {}, {}, {}
-        shared = {(1, 0): "raw12_384", (1, 1): "raw12_0"}
         for b in range(3):
-            h_scales[b] = keep.tile([P, S], U8, name=f"h_scales{b}", align_bytes=64)
+            for h in range(2):
+                h_scales[b, h] = keep.tile([P, HALF], U8, name=f"h_scales{b}{h}", align_bytes=64)
 
-        def relu(engine, b, h, bank):
-            name = shared.get((b, h), f"h_grouped{b}{h}")
-            tile = keep.tile([P, HALF, 4], BF16, name=name, align_bytes=64)
-            src = bank[:].rearrange("p t n -> p n t")
+        def relu(engine, b, h):
+            shared = {(first, 0): f"raw{second}0_0", (first, 1): f"raw{second}1_0", (second, 0): f"raw{last}1_384"}
+            tile = keep.tile([P, HALF, 4], BF16, name=shared.get((b, h), f"h_grouped{b}{h}"), align_bytes=64)
+            src = banks[b, h][:].rearrange("p t n -> p n t")
             if engine is nc.scalar:
                 nc.scalar.activation(tile[:], src, RELU)
             else:
                 nc.vector.tensor_scalar_max(tile[:], src, 0.0)
             h_grouped[b, h] = tile
 
-        def hidden_quantise(b):
-            h_codes[b] = keep.tile([P, S], U32, name="grouped21" if b == 1 else f"h_codes{b}", align_bytes=64)
-            for h in range(2):
-                toks = slice(HALF * h, HALF * (h + 1))
-                nc.vector.quantize_mx(
-                    out=h_codes[b][:, toks].bitcast(FP8),
-                    scales=h_scales[b][:, toks],
-                    in_=h_grouped[b, h][:].rearrange("p n t -> p (n t)"),
-                )
+        def hidden_quantise(b, h):
+            if b != last:
+                if h == 0:
+                    name = f"grouped{second}11" if b == first else f"grouped{last}11"
+                    h_codes[b] = keep.tile([P, S], U32, name=name, align_bytes=64)
+                h_codes[b, h] = h_codes[b][:, HALF * h : HALF * (h + 1)]
+            else:
+                tile = keep.tile([P, HALF], U32, name=f"h_codes{b}{h}", align_bytes=64)
+                h_codes[b, h] = tile[:]
+            nc.vector.quantize_mx(
+                out=h_codes[b, h].bitcast(FP8),
+                scales=h_scales[b, h][:],
+                in_=h_grouped[b, h][:].rearrange("p n t -> p (n t)"),
+            )
 
-        def out_matmul(acc, m, h, b):
+        acc = {}
+
+        def out_matmul(m, h, b, start, stop):
             if b == 0:
                 lhsT = w8_codes[:, HALF * m : HALF * (m + 1)].bitcast(FP8)
             else:
                 lhsT = w4_codes[:, b - 1, 64 * m : 64 * (m + 1)].bitcast(FP4)
             nc.tensor.matmul_mx(
-                out=acc[:],
+                out=acc[m, h],
                 lhsT=lhsT,
                 lhsT_scale=w2_scales[:, b, 32 * m : 32 * (m + 1)].bitcast(U8),
-                rhs=h_codes[b][:, HALF * h : HALF * (h + 1)].bitcast(FP8),
-                rhs_scale=h_scales[b][:, HALF * h : HALF * (h + 1)],
-                start=b == 0,
-                stop=b == 2,
+                rhs=h_codes[b, h].bitcast(FP8),
+                rhs_scale=h_scales[b, h][:],
+                start=start,
+                stop=stop,
             )
 
-        acc = {}
+        in_order = [(a, t) for a in range(2) for t in range(4)]
+        whole_block(first, 0)
+        whole_block(first, 1)
+        hidden_matmuls(first, in_order)
+        whole_block(second, 0)
+        relu(nc.scalar, first, 0)
+        whole_block(second, 1)
+        relu(nc.scalar, first, 1)
+        hidden_matmuls(second, in_order[4:6] + in_order[0:4] + in_order[6:8])
+        hidden_quantise(first, 0)
+        hidden_quantise(first, 1)
+        interleave(nc.scalar, last, 0, 0, 1, 0, 128)
+        interleave(nc.vector, last, 0, 0, 0, 0, 128)
+        quantise(last, 0, 0, 0, 1024)
+        for c0, m0, m1 in ((0, 0, 64), (256, 64, 96), (384, 96, 128)):
+            interleave(nc.scalar, last, 1, c0, 1, m0, m1)
+            interleave(nc.vector, last, 1, c0, 0, m0, m1)
+        quantise(last, 0, 1, 0, 1024)
+        for g in range(2):
+            for u in range(2):
+                for t in range(2):
+                    quantise(last, 1, u, 512 * t + 256 * g, 512 * t + 256 * (g + 1))
+        relu(nc.scalar, second, 0)
+        relu(nc.scalar, second, 1)
+        hidden_matmuls(last, in_order)
+        hidden_quantise(second, 0)
+        hidden_quantise(second, 1)
 
-        def start_out(m, h, name):
-            acc[m, h] = psum.tile([P, HALF], F32, name=name)
-            out_matmul(acc[m, h], m, h, 0)
-
-        def finish_out(m):
-            res = keep.tile([P, S], F32, name=f"res{m}")
-            for h in range(2):
-                out_matmul(acc[m, h], m, h, 2)
-                toks = slice(HALF * h, HALF * (h + 1))
-                nc.vector.tensor_add(res[:, toks], acc[m, h][:], prev_sb[:, m, toks])
-                if m == 3:
-                    queue = nc.scalar if h == 0 else nc.sync
-                    queue.dma_start(out[P * m : P * (m + 1), toks], res[:, toks])
-            if m < 3:
-                queue = nc.scalar if m == 1 else nc.sync
-                queue.dma_start(out[P * m : P * (m + 1), :], res[:])
-
-        interleave(0, 0)
-        quantise(0, 0, 1024)
-        interleave(0, 1)
-        quantise(0, 1, 1024)
-        banks = hidden_matmuls(0)
-        interleave(1, 0)
-        quantise(1, 0, 1024)
-        interleave(1, 1)
-        relu(nc.scalar, 0, 0, banks[0])
-        relu(nc.vector, 0, 1, banks[1])
-        quantise(1, 1, 1024)
-        banks = hidden_matmuls(1)
-        hidden_quantise(0)
-        interleave(2, 0)
-        quantise(2, 0, 1024)
-        interleave(2, 1)
-        quantise(2, 1, 512)
-        relu(nc.scalar, 1, 0, banks[0])
-        relu(nc.scalar, 1, 1, banks[1])
-        hidden_quantise(1)
-        banks = hidden_matmuls(2)
-        for m in range(2):
-            for h in range(2):
-                start_out(m, h, f"acc{m}{h}")
-        for h in range(2):
-            start_out(2, h, f"hidden1{h}")
-        for m in range(3):
-            for h in range(2):
-                out_matmul(acc[m, h], m, h, 1)
-        relu(nc.scalar, 2, 0, banks[0])
-        relu(nc.vector, 2, 1, banks[1])
-        for h in range(2):
-            start_out(3, h, f"hidden0{h}")
-            out_matmul(acc[3, h], 3, h, 1)
-        hidden_quantise(2)
+        outs = [psum.tile([P, S], F32, name=f"out{m}") for m in range(4)]
         for m in range(4):
-            finish_out(m)
+            for h in range(2):
+                acc[m, h] = outs[m][:, HALF * h : HALF * (h + 1)]
+        for h in range(2):
+            for b in (second, first):
+                for m in range(4):
+                    out_matmul(m, h, b, b == second and h == 0, False)
+        relu(nc.scalar, last, 0)
+        relu(nc.vector, last, 1)
+        hidden_quantise(last, 0)
+        hidden_quantise(last, 1)
+        for m in range(4):
+            for h in range(2):
+                out_matmul(m, h, last, False, h == 1)
+        for m in range(4):
+            result = keep.tile([P, S], F32, name=f"result{m}")
+            nc.vector.tensor_add(result[:], outs[m][:], prev_sb[:, m, :])
+            queue = nc.scalar if m % 2 == 0 else nc.sync
+            queue.dma_start(out[P * m : P * (m + 1), :], result[:])

@@ -33,7 +33,7 @@ def tile_list_tabmlp_mix_res_kernel(
         table_scales = keep.tile([P, T // 4], I32, name="table_scales", align_bytes=64)
         w2_scales = keep.tile([P, 3, M // 4], I32, name="w2_scales", align_bytes=64)
         w8_codes = keep.tile([P, M], I32, name="w8_codes", align_bytes=64)
-        w4_codes = keep.tile([P, 2, M // 2], I32, name="w4_codes", align_bytes=64)
+        w4_codes = [keep.tile([P, M // 2], I32, name=f"w4_codes{a}", align_bytes=64) for a in range(2)]
         prev_sb = keep.tile([P, 4, S], F32, name="prev_sb")
 
         nc.vector.memset(table_scales[:], 0)
@@ -74,7 +74,8 @@ def tile_list_tabmlp_mix_res_kernel(
         load_w1(last, 1, 0, 256)
         load_w1(last, 1, 256, 384)
         load_w1(last, 1, 384, 512)
-        nc.sync.dma_start(w4_codes[:], w4_words.bitcast(I32).rearrange("a p c -> p a c"))
+        nc.sync.dma_start(w4_codes[first - 1][:], w4_words.bitcast(I32)[first - 1])
+        nc.sync.dma_start(w4_codes[second - 1][:], w4_words.bitcast(I32)[second - 1])
         nc.sync.dma_start(w8_codes[:], w8_words[0].rearrange("p n i -> p (n i)").bitcast(I32))
         nc.sync.dma_start(prev_sb[:], prev.rearrange("(m p) j -> p m j", p=P))
 
@@ -110,9 +111,15 @@ def tile_list_tabmlp_mix_res_kernel(
                 out=codes[b, a][:, o].bitcast(FP8), scales=scales[b, a][:, o], in_=grouped[b, a, u][:, i0:i1]
             )
 
+        def split(b, a, c0, m0, m1, cut):
+            if m0 + cut < m1:
+                interleave(nc.scalar, b, a, c0, 1, m0 + cut, m1)
+            interleave(nc.vector, b, a, c0, 0, m0, m1)
+            if cut:
+                interleave(nc.vector, b, a, c0, 1, m0, m0 + cut)
+
         def whole_block(b, a):
-            interleave(nc.scalar, b, a, 0, 1, 0, 128)
-            interleave(nc.vector, b, a, 0, 0, 0, 128)
+            split(b, a, 0, 0, 128, 16)
             quantise(b, a, 0, 0, 1024)
             quantise(b, a, 1, 0, 1024)
 
@@ -121,63 +128,63 @@ def tile_list_tabmlp_mix_res_kernel(
         def hidden_matmuls(b, steps):
             for h in range(2):
                 banks[b, h] = psum.tile([P, 4, HALF], F32, name=f"hidden{int(b == second)}{h}")
-            for a, t in steps:
+            passes = [(a, t, h) for a, t in steps for h in range(2)]
+            if b == last:
+                passes = passes[:8] + passes[8::2] + passes[9::2]
+            for a, t, h in passes:
                 cols = slice(HALF * t, HALF * (t + 1))
-                for h in range(2):
-                    toks = slice(HALF * h, HALF * (h + 1))
-                    nc.tensor.matmul_mx(
-                        out=banks[b, h][:, t, :],
-                        lhsT=codes[b, a][:, cols].bitcast(FP8),
-                        lhsT_scale=scales[b, a][:, cols],
-                        rhs=picked_words[a][:, toks].bitcast(FP8),
-                        rhs_scale=picked_scales[4 * a : P, toks],
-                        start=(a, t) == steps[0],
-                        stop=(a, t) == steps[-1],
-                    )
+                toks = slice(HALF * h, HALF * (h + 1))
+                nc.tensor.matmul_mx(
+                    out=banks[b, h][:, t, :],
+                    lhsT=codes[b, a][:, cols].bitcast(FP8),
+                    lhsT_scale=scales[b, a][:, cols],
+                    rhs=picked_words[a][:, toks].bitcast(FP8),
+                    rhs_scale=picked_scales[4 * a : P, toks],
+                    start=(a, t) == steps[0],
+                    stop=(a, t) == steps[-1],
+                )
 
         h_grouped, h_codes, h_scales = {}, {}, {}
         for b in range(3):
-            for h in range(2):
-                h_scales[b, h] = keep.tile([P, HALF], U8, name=f"h_scales{b}{h}", align_bytes=64)
+            h_scales[b] = keep.tile([P, S], U8, name=f"h_scales{b}", align_bytes=64)
 
         def relu(engine, b, h):
-            shared = {(first, 0): f"raw{second}0_0", (first, 1): f"raw{second}1_0", (second, 0): f"raw{last}1_384"}
-            tile = keep.tile([P, HALF, 4], BF16, name=shared.get((b, h), f"h_grouped{b}{h}"), align_bytes=64)
+            shared = {
+                (first, 0): f"raw{second}0_0",
+                (first, 1): f"raw{second}1_0",
+                (second, 0): f"raw{last}1_0",
+                (second, 1): f"raw{last}1_384",
+            }
+            tile = keep.tile([P, HALF, 4], BF16, name=shared.get((b, h), f"h_grouped{h}"), align_bytes=64)
+            h_grouped[b, h] = tile[:]
             src = banks[b, h][:].rearrange("p t n -> p n t")
             if engine is nc.scalar:
-                nc.scalar.activation(tile[:], src, RELU)
+                nc.scalar.activation(h_grouped[b, h], src, RELU)
             else:
-                nc.vector.tensor_scalar_max(tile[:], src, 0.0)
-            h_grouped[b, h] = tile
+                nc.vector.tensor_scalar_max(h_grouped[b, h], src, 0.0)
 
         def hidden_quantise(b, h):
-            if b != last:
-                if h == 0:
-                    name = f"grouped{second}11" if b == first else f"grouped{last}11"
-                    h_codes[b] = keep.tile([P, S], U32, name=name, align_bytes=64)
-                h_codes[b, h] = h_codes[b][:, HALF * h : HALF * (h + 1)]
-            else:
-                tile = keep.tile([P, HALF], U32, name=f"h_codes{b}{h}", align_bytes=64)
-                h_codes[b, h] = tile[:]
+            if h == 0:
+                name = {first: f"grouped{second}11", second: f"grouped{last}11", last: "h_codes_last"}[b]
+                h_codes[b] = keep.tile([P, S], U32, name=name, align_bytes=64)
+            toks = slice(HALF * h, HALF * (h + 1))
             nc.vector.quantize_mx(
-                out=h_codes[b, h].bitcast(FP8),
-                scales=h_scales[b, h][:],
-                in_=h_grouped[b, h][:].rearrange("p n t -> p (n t)"),
+                out=h_codes[b][:, toks].bitcast(FP8),
+                scales=h_scales[b][:, toks],
+                in_=h_grouped[b, h].rearrange("p n t -> p (n t)"),
             )
 
-        acc = {}
-
-        def out_matmul(m, h, b, start, stop):
+        def out_matmul(m, toks, b, start, stop):
             if b == 0:
                 lhsT = w8_codes[:, HALF * m : HALF * (m + 1)].bitcast(FP8)
             else:
-                lhsT = w4_codes[:, b - 1, 64 * m : 64 * (m + 1)].bitcast(FP4)
+                lhsT = w4_codes[b - 1][:, 64 * m : 64 * (m + 1)].bitcast(FP4)
             nc.tensor.matmul_mx(
-                out=acc[m, h],
+                out=outs[m][:, toks],
                 lhsT=lhsT,
                 lhsT_scale=w2_scales[:, b, 32 * m : 32 * (m + 1)].bitcast(U8),
-                rhs=h_codes[b, h].bitcast(FP8),
-                rhs_scale=h_scales[b, h][:],
+                rhs=h_codes[b][:, toks].bitcast(FP8),
+                rhs_scale=h_scales[b][:, toks],
                 start=start,
                 stop=stop,
             )
@@ -193,38 +200,39 @@ def tile_list_tabmlp_mix_res_kernel(
         hidden_matmuls(second, in_order[4:6] + in_order[0:4] + in_order[6:8])
         hidden_quantise(first, 0)
         hidden_quantise(first, 1)
-        interleave(nc.scalar, last, 0, 0, 1, 0, 128)
-        interleave(nc.vector, last, 0, 0, 0, 0, 128)
+        split(last, 0, 0, 0, 128, 16)
         quantise(last, 0, 0, 0, 1024)
-        for c0, m0, m1 in ((0, 0, 64), (256, 64, 96), (384, 96, 128)):
-            interleave(nc.scalar, last, 1, c0, 1, m0, m1)
-            interleave(nc.vector, last, 1, c0, 0, m0, m1)
         quantise(last, 0, 1, 0, 1024)
-        for g in range(2):
-            for u in range(2):
-                for t in range(2):
-                    quantise(last, 1, u, 512 * t + 256 * g, 512 * t + 256 * (g + 1))
+        split(last, 1, 0, 0, 64, 0)
         relu(nc.scalar, second, 0)
+        split(last, 1, 256, 64, 96, 32)
+        for t in range(2):
+            quantise(last, 1, 0, 512 * t + 0, 512 * t + 256)
+        split(last, 1, 384, 96, 128, 0)
+        for t in range(2):
+            quantise(last, 1, 1, 512 * t + 0, 512 * t + 256)
+        for t in range(2):
+            quantise(last, 1, 0, 512 * t + 256, 512 * t + 512)
+        for t in range(2):
+            quantise(last, 1, 1, 512 * t + 256, 512 * t + 512)
         relu(nc.scalar, second, 1)
         hidden_matmuls(last, in_order)
         hidden_quantise(second, 0)
         hidden_quantise(second, 1)
 
         outs = [psum.tile([P, S], F32, name=f"out{m}") for m in range(4)]
-        for m in range(4):
-            for h in range(2):
-                acc[m, h] = outs[m][:, HALF * h : HALF * (h + 1)]
+        halves = [slice(0, HALF), slice(HALF, S)]
+        early = [(first, 0), (second, 0), (first, 1), (second, 1)]
+        for b, h in early:
+            for m in range(4):
+                out_matmul(m, halves[h], b, (b, h) == early[0], False)
+        relu(nc.vector, last, 0)
+        relu(nc.scalar, last, 1)
         for h in range(2):
-            for b in (second, first):
-                for m in range(4):
-                    out_matmul(m, h, b, b == second and h == 0, False)
-        relu(nc.scalar, last, 0)
-        relu(nc.vector, last, 1)
-        hidden_quantise(last, 0)
-        hidden_quantise(last, 1)
-        for m in range(4):
-            for h in range(2):
-                out_matmul(m, h, last, False, h == 1)
+            hidden_quantise(last, h)
+        for h in range(2):
+            for m in range(4):
+                out_matmul(m, halves[h], last, False, h == 1)
         for m in range(4):
             result = keep.tile([P, S], F32, name=f"result{m}")
             nc.vector.tensor_add(result[:], outs[m][:], prev_sb[:, m, :])

@@ -29,7 +29,7 @@ def tile_list_tabmlp_mix_res_kernel(
         psum = ctx.enter_context(tc.psum_pool(name="psum", bufs=1))
 
         offsets = keep.tile([P, S // 16], U16, name="offsets")
-        table_words = [keep.tile([P, T], I32, name=f"table_words{a}", align_bytes=64) for a in range(2)]
+        table_words = keep.tile([P, 2, T], I32, name="table_words", align_bytes=64)
         table_scales = keep.tile([P, T // 4], I32, name="table_scales", align_bytes=64)
         w2_scales = keep.tile([P, 3, M // 4], I32, name="w2_scales", align_bytes=64)
         w8_codes = keep.tile([P, M], I32, name="w8_codes", align_bytes=64)
@@ -53,10 +53,7 @@ def tile_list_tabmlp_mix_res_kernel(
         w8_rows = w8_scales.bitcast(I32)
         w4_rows = w4_scales.bitcast(I32)
 
-        for a in range(2):
-            nc.sync.dma_start(
-                table_words[a][:], tab_i32[a, 0 : WORD_BYTES // 4].rearrange("(p c) -> p c", p=P)
-            )
+        nc.sync.dma_start(table_words[:], tab_i32[:, 0 : WORD_BYTES // 4].rearrange("a (p c) -> p a c", p=P))
         nc.sync.dma_start(offsets[:], offs)
         for q in range(4):
             nc.sync.dma_start(table_scales[32 * q : 32 * q + 8, :], tab_scale_rows[:, 4 * q : 4 * q + 4, :])
@@ -82,7 +79,7 @@ def tile_list_tabmlp_mix_res_kernel(
         picked_words = []
         for a in range(2):
             words = keep.tile([P, S], U32, name=f"picked_words{a}", align_bytes=64)
-            nc.vector.tensor_copy(words[:], table_words[a][:].bitcast(U32).indirect(offsets[:]))
+            nc.vector.tensor_copy(words[:], table_words[:, a, :].bitcast(U32).indirect(offsets[:]))
             picked_words.append(words)
         picked_scales = keep.tile([P, S], U8, name="picked_scales", align_bytes=64)
         nc.vector.tensor_copy(picked_scales[:], table_scales[:].bitcast(U8).indirect(offsets[:]))
@@ -180,7 +177,7 @@ def tile_list_tabmlp_mix_res_kernel(
             else:
                 lhsT = w4_codes[b - 1][:, 64 * m : 64 * (m + 1)].bitcast(FP4)
             nc.tensor.matmul_mx(
-                out=outs[m][:, toks],
+                out=outs[m, toks.start // HALF],
                 lhsT=lhsT,
                 lhsT_scale=w2_scales[:, b, 32 * m : 32 * (m + 1)].bitcast(U8),
                 rhs=h_codes[b][:, toks].bitcast(FP8),
@@ -200,12 +197,12 @@ def tile_list_tabmlp_mix_res_kernel(
         hidden_matmuls(second, in_order[4:6] + in_order[0:4] + in_order[6:8])
         hidden_quantise(first, 0)
         hidden_quantise(first, 1)
-        split(last, 0, 0, 0, 128, 16)
+        split(last, 0, 0, 0, 128, 24)
         quantise(last, 0, 0, 0, 1024)
         quantise(last, 0, 1, 0, 1024)
         split(last, 1, 0, 0, 64, 0)
         relu(nc.scalar, second, 0)
-        split(last, 1, 256, 64, 96, 32)
+        split(last, 1, 256, 64, 96, 16)
         for t in range(2):
             quantise(last, 1, 0, 512 * t + 0, 512 * t + 256)
         split(last, 1, 384, 96, 128, 0)
@@ -220,21 +217,27 @@ def tile_list_tabmlp_mix_res_kernel(
         hidden_quantise(second, 0)
         hidden_quantise(second, 1)
 
-        outs = [psum.tile([P, S], F32, name=f"out{m}") for m in range(4)]
+        whole = [psum.tile([P, S], F32, name=f"out{m}") for m in range(1, 4)]
+        outs = {(m, h): whole[m - 1][:, HALF * h : HALF * (h + 1)] for m in range(1, 4) for h in range(2)}
+        outs[0, 0] = psum.tile([P, HALF], F32, name="out0")[:]
+        outs[0, 1] = psum.tile([P, HALF], F32, name="hidden10")[:]
         halves = [slice(0, HALF), slice(HALF, S)]
-        early = [(first, 0), (second, 0), (first, 1), (second, 1)]
-        for b, h in early:
+        for b, h in ((first, 0), (second, 0), (second, 1), (first, 1)):
             for m in range(4):
-                out_matmul(m, halves[h], b, (b, h) == early[0], False)
-        relu(nc.vector, last, 0)
-        relu(nc.scalar, last, 1)
+                out_matmul(m, halves[h], b, (b, h) == (first, 0) or (m, b, h) == (0, second, 1), False)
+        relu(nc.scalar, last, 0)
+        relu(nc.vector, last, 1)
         for h in range(2):
             hidden_quantise(last, h)
         for h in range(2):
             for m in range(4):
-                out_matmul(m, halves[h], last, False, h == 1)
-        for m in range(4):
+                out_matmul(m, halves[h], last, False, h == 1 or m == 0)
+        for h in range(2):
+            part = keep.tile([P, HALF], F32, name=f"part{h}")
+            nc.vector.tensor_add(part[:], outs[0, h], prev_sb[:, 0, halves[h]])
+            nc.sync.dma_start(out[0:P, halves[h]], part[:])
+        for m in range(1, 4):
             result = keep.tile([P, S], F32, name=f"result{m}")
-            nc.vector.tensor_add(result[:], outs[m][:], prev_sb[:, m, :])
-            queue = nc.scalar if m % 2 == 0 else nc.sync
+            nc.vector.tensor_add(result[:], whole[m - 1][:], prev_sb[:, m, :])
+            queue = nc.scalar if m % 2 == 1 else nc.sync
             queue.dma_start(out[P * m : P * (m + 1), :], result[:])

@@ -29,7 +29,7 @@ def tile_list_tabmlp_mix_res_kernel(
         psum = ctx.enter_context(tc.psum_pool(name="psum", bufs=1))
 
         offsets = keep.tile([P, S // 16], U16, name="offsets")
-        table_words = keep.tile([P, 2, T], I32, name="table_words", align_bytes=64)
+        table_words = [keep.tile([P, T], I32, name=f"table_words{a}", align_bytes=64) for a in range(2)]
         table_scales = keep.tile([P, T // 4], I32, name="table_scales", align_bytes=64)
         w2_scales = keep.tile([P, 3, M // 4], I32, name="w2_scales", align_bytes=64)
         w8_codes = keep.tile([P, M], I32, name="w8_codes", align_bytes=64)
@@ -53,11 +53,14 @@ def tile_list_tabmlp_mix_res_kernel(
         w8_rows = w8_scales.bitcast(I32)
         w4_rows = w4_scales.bitcast(I32)
 
-        nc.sync.dma_start(table_words[:], tab_i32[:, 0 : WORD_BYTES // 4].rearrange("a (p c) -> p a c", p=P))
+        for a in range(2):
+            nc.sync.dma_start(
+                table_words[a][:], tab_i32[a, 0 : WORD_BYTES // 4].rearrange("(p c) -> p c", p=P)
+            )
         nc.sync.dma_start(offsets[:], offs)
+        load_w1(first, 0, 0, 512)
         for q in range(4):
             nc.sync.dma_start(table_scales[32 * q : 32 * q + 8, :], tab_scale_rows[:, 4 * q : 4 * q + 4, :])
-        load_w1(first, 0, 0, 512)
         load_w1(first, 1, 0, 512)
         for q in range(4):
             nc.sync.dma_start(
@@ -79,7 +82,7 @@ def tile_list_tabmlp_mix_res_kernel(
         picked_words = []
         for a in range(2):
             words = keep.tile([P, S], U32, name=f"picked_words{a}", align_bytes=64)
-            nc.vector.tensor_copy(words[:], table_words[:, a, :].bitcast(U32).indirect(offsets[:]))
+            nc.vector.tensor_copy(words[:], table_words[a][:].bitcast(U32).indirect(offsets[:]))
             picked_words.append(words)
         picked_scales = keep.tile([P, S], U8, name="picked_scales", align_bytes=64)
         nc.vector.tensor_copy(picked_scales[:], table_scales[:].bitcast(U8).indirect(offsets[:]))

@@ -29,12 +29,12 @@ def tile_list_tabmlp_mix_res_kernel(
         psum = ctx.enter_context(tc.psum_pool(name="psum", bufs=1))
 
         offsets = keep.tile([P, S // 16], U16, name="offsets")
-        table_words = [keep.tile([P, T], I32, name=f"table_words{a}", align_bytes=64) for a in range(2)]
-        table_scales = keep.tile([P, T // 4], I32, name="table_scales", align_bytes=64)
-        w2_scales = keep.tile([P, 3, M // 4], I32, name="w2_scales", align_bytes=64)
-        w8_codes = keep.tile([P, M], I32, name="w8_codes", align_bytes=64)
-        w4_codes = [keep.tile([P, M // 2], I32, name=f"w4_codes{a}", align_bytes=64) for a in range(2)]
-        prev_sb = keep.tile([P, 4, S], F32, name="prev_sb")
+        table_words = [keep.tile([P, T], I32, name=f"table_words{a}", align_bytes=256) for a in range(2)]
+        table_scales = keep.tile([P, T // 4], I32, name="table_scales", align_bytes=256)
+        w2_scales = keep.tile([P, 3, M // 4], I32, name="w2_scales", align_bytes=256)
+        w8_codes = keep.tile([P, M], I32, name="w8_codes", align_bytes=256)
+        w4_codes = [keep.tile([P, M // 2], I32, name=f"w4_codes{a}", align_bytes=256) for a in range(2)]
+        prev_sb = keep.tile([P, 4, S], F32, name="prev_sb", align_bytes=256)
 
         nc.vector.memset(table_scales[:], 0)
         nc.vector.memset(w2_scales[:], 0)
@@ -43,7 +43,7 @@ def tile_list_tabmlp_mix_res_kernel(
         first, second, last = 1, 2, 0
 
         def load_w1(b, a, c0, c1):
-            raw = keep.tile([P, 4, c1 - c0], F32, name=f"raw{b}{a}_{c0}", align_bytes=64)
+            raw = keep.tile([P, 4, c1 - c0], F32, name=f"raw{b}{a}_{c0}", align_bytes=256)
             rows = w1[512 * a : 512 * (a + 1), 512 * b + c0 : 512 * b + c1]
             nc.sync.dma_start(raw[:], rows.rearrange("(p j) c -> p j c", j=4))
             raws[b, a, c0] = raw
@@ -81,19 +81,19 @@ def tile_list_tabmlp_mix_res_kernel(
 
         picked_words = []
         for a in range(2):
-            words = keep.tile([P, S], U32, name=f"picked_words{a}", align_bytes=64)
+            words = keep.tile([P, S], U32, name=f"picked_words{a}", align_bytes=256)
             nc.vector.tensor_copy(words[:], table_words[a][:].bitcast(U32).indirect(offsets[:]))
             picked_words.append(words)
-        picked_scales = keep.tile([P, S], U8, name="picked_scales", align_bytes=64)
+        picked_scales = keep.tile([P, S], U8, name="picked_scales", align_bytes=256)
         nc.vector.tensor_copy(picked_scales[:], table_scales[:].bitcast(U8).indirect(offsets[:]))
 
         grouped, codes, scales = {}, {}, {}
         for b in range(3):
             for a in range(2):
                 for u in range(2):
-                    grouped[b, a, u] = keep.tile([P, 1024], BF16, name=f"grouped{b}{a}{u}", align_bytes=64)
-                codes[b, a] = keep.tile([P, 512], U32, name=f"w1_codes{b}{a}", align_bytes=64)
-                scales[b, a] = keep.tile([P, 512], U8, name=f"w1_scales{b}{a}", align_bytes=64)
+                    grouped[b, a, u] = keep.tile([P, 1024], BF16, name=f"grouped{b}{a}{u}", align_bytes=256)
+                codes[b, a] = keep.tile([P, 512], U32, name=f"w1_codes{b}{a}", align_bytes=256)
+                scales[b, a] = keep.tile([P, 512], U8, name=f"w1_scales{b}{a}", align_bytes=256)
 
         def interleave(engine, b, a, c0, u, m0, m1):
             view = grouped[b, a, u][:].rearrange("p (t m j) -> p m j t", t=2, j=4)
@@ -146,7 +146,7 @@ def tile_list_tabmlp_mix_res_kernel(
 
         h_grouped, h_codes, h_scales = {}, {}, {}
         for b in range(3):
-            h_scales[b] = keep.tile([P, S], U8, name=f"h_scales{b}", align_bytes=64)
+            h_scales[b] = keep.tile([P, S], U8, name=f"h_scales{b}", align_bytes=256)
 
         def relu(engine, b, h):
             shared = {
@@ -155,7 +155,7 @@ def tile_list_tabmlp_mix_res_kernel(
                 (second, 0): f"raw{last}1_0",
                 (second, 1): f"raw{last}1_384",
             }
-            tile = keep.tile([P, HALF, 4], BF16, name=shared.get((b, h), f"h_grouped{h}"), align_bytes=64)
+            tile = keep.tile([P, HALF, 4], BF16, name=shared.get((b, h), f"h_grouped{h}"), align_bytes=256)
             h_grouped[b, h] = tile[:]
             src = banks[b, h][:].rearrange("p t n -> p n t")
             if engine is nc.scalar:
@@ -166,7 +166,7 @@ def tile_list_tabmlp_mix_res_kernel(
         def hidden_quantise(b, h):
             if h == 0:
                 name = {first: f"grouped{second}11", second: f"grouped{last}11", last: "h_codes_last"}[b]
-                h_codes[b] = keep.tile([P, S], U32, name=name, align_bytes=64)
+                h_codes[b] = keep.tile([P, S], U32, name=name, align_bytes=256)
             toks = slice(HALF * h, HALF * (h + 1))
             nc.vector.quantize_mx(
                 out=h_codes[b][:, toks].bitcast(FP8),
@@ -236,11 +236,11 @@ def tile_list_tabmlp_mix_res_kernel(
             for m in range(4):
                 out_matmul(m, halves[h], last, False, h == 1 or m == 0)
         for h in range(2):
-            part = keep.tile([P, HALF], F32, name=f"part{h}")
+            part = keep.tile([P, HALF], F32, name=f"part{h}", align_bytes=256)
             nc.vector.tensor_add(part[:], outs[0, h], prev_sb[:, 0, halves[h]])
             nc.sync.dma_start(out[0:P, halves[h]], part[:])
         for m in range(1, 4):
-            result = keep.tile([P, S], F32, name=f"result{m}")
+            result = keep.tile([P, S], F32, name=f"result{m}", align_bytes=256)
             nc.vector.tensor_add(result[:], whole[m - 1][:], prev_sb[:, m, :])
             queue = nc.scalar if m % 2 == 1 else nc.sync
             queue.dma_start(out[P * m : P * (m + 1), :], result[:])

@@ -67,8 +67,6 @@ def tile_list_tabmlp_mix_res_kernel(
                 w2_scales[32 * q : 32 * q + 4, 1:3, :], w4_rows[:, 4 * q : 4 * q + 4, :].rearrange("a q c -> q a c")
             )
         load_w1(second, 0, 0, 512)
-        for q in range(4):
-            nc.sync.dma_start(w2_scales[32 * q : 32 * q + 4, 0, :], w8_rows[0, 4 * q : 4 * q + 4, :])
         load_w1(second, 1, 0, 512)
         load_w1(last, 0, 0, 512)
         load_w1(last, 1, 0, 256)
@@ -78,6 +76,8 @@ def tile_list_tabmlp_mix_res_kernel(
         nc.sync.dma_start(w4_codes[second - 1][:], w4_words.bitcast(I32)[second - 1])
         nc.sync.dma_start(w8_codes[:], w8_words[0].rearrange("p n i -> p (n i)").bitcast(I32))
         nc.sync.dma_start(prev_sb[:], prev.rearrange("(m p) j -> p m j", p=P))
+        for q in range(4):
+            nc.sync.dma_start(w2_scales[32 * q : 32 * q + 4, 0, :], w8_rows[0, 4 * q : 4 * q + 4, :])
 
         picked_words = []
         for a in range(2):

@@ -119,7 +119,7 @@ def tile_list_tabmlp_mix_res_kernel(
                 interleave(nc.vector, b, a, c0, 1, m0, m0 + cut)
 
         def whole_block(b, a):
-            split(b, a, 0, 0, 128, 16)
+            split(b, a, 0, 0, 128, 32)
             quantise(b, a, 0, 0, 1024)
             quantise(b, a, 1, 0, 1024)
 
@@ -180,7 +180,7 @@ def tile_list_tabmlp_mix_res_kernel(
             else:
                 lhsT = w4_codes[b - 1][:, 64 * m : 64 * (m + 1)].bitcast(FP4)
             nc.tensor.matmul_mx(
-                out=outs[m, toks.start // HALF],
+                out=outs[m, toks.start // HALF] if toks.stop - toks.start == HALF else whole[m - 1][:],
                 lhsT=lhsT,
                 lhsT_scale=w2_scales[:, b, 32 * m : 32 * (m + 1)].bitcast(U8),
                 rhs=h_codes[b][:, toks].bitcast(FP8),
@@ -200,10 +200,10 @@ def tile_list_tabmlp_mix_res_kernel(
         hidden_matmuls(second, in_order[4:6] + in_order[0:4] + in_order[6:8])
         hidden_quantise(first, 0)
         hidden_quantise(first, 1)
-        split(last, 0, 0, 0, 128, 24)
+        split(last, 0, 0, 0, 128, 48)
         quantise(last, 0, 0, 0, 1024)
         quantise(last, 0, 1, 0, 1024)
-        split(last, 1, 0, 0, 64, 0)
+        split(last, 1, 0, 0, 64, 16)
         relu(nc.scalar, second, 0)
         split(last, 1, 256, 64, 96, 16)
         for t in range(2):
@@ -233,8 +233,9 @@ def tile_list_tabmlp_mix_res_kernel(
         for h in range(2):
             hidden_quantise(last, h)
         for h in range(2):
-            for m in range(4):
-                out_matmul(m, halves[h], last, False, h == 1 or m == 0)
+            out_matmul(0, halves[h], last, False, True)
+        for m in range(1, 4):
+            out_matmul(m, slice(0, S), last, False, True)
         for h in range(2):
             part = keep.tile([P, HALF], F32, name=f"part{h}", align_bytes=256)
             nc.vector.tensor_add(part[:], outs[0, h], prev_sb[:, 0, halves[h]])

@@ -30,7 +30,7 @@ def tile_list_tabmlp_mix_res_kernel(
 
         offsets = keep.tile([P, S // 16], U16, name="offsets")
         table_words = [keep.tile([P, T], I32, name=f"table_words{a}", align_bytes=256) for a in range(2)]
-        table_scales = keep.tile([P, T // 4], I32, name="table_scales", align_bytes=256)
+        table_scales = keep.tile([P, 2, T // 4], I32, name="table_scales", align_bytes=256)
         w2_scales = keep.tile([P, 3, M // 4], I32, name="w2_scales", align_bytes=256)
         w8_codes = keep.tile([P, M], I32, name="w8_codes", align_bytes=256)
         w4_codes = [keep.tile([P, M // 2], I32, name=f"w4_codes{a}", align_bytes=256) for a in range(2)]
@@ -60,32 +60,38 @@ def tile_list_tabmlp_mix_res_kernel(
         nc.sync.dma_start(offsets[:], offs)
         load_w1(first, 0, 0, 512)
         for q in range(4):
-            nc.sync.dma_start(table_scales[32 * q : 32 * q + 8, :], tab_scale_rows[:, 4 * q : 4 * q + 4, :])
-        load_w1(first, 1, 0, 512)
-        for q in range(4):
             nc.sync.dma_start(
-                w2_scales[32 * q : 32 * q + 4, 1:3, :], w4_rows[:, 4 * q : 4 * q + 4, :].rearrange("a q c -> q a c")
+                table_scales[32 * q : 32 * q + 4],
+                tab_scale_rows[:, 4 * q : 4 * q + 4, :].rearrange("a q c -> q a c"),
             )
+        load_w1(first, 1, 0, 512)
         load_w1(second, 0, 0, 512)
         load_w1(second, 1, 0, 512)
         load_w1(last, 0, 0, 512)
         load_w1(last, 1, 0, 256)
         load_w1(last, 1, 256, 384)
         load_w1(last, 1, 384, 512)
+        for q in range(4):
+            nc.sync.dma_start(
+                w2_scales[32 * q : 32 * q + 4, 1:3, :], w4_rows[:, 4 * q : 4 * q + 4, :].rearrange("a q c -> q a c")
+            )
         nc.sync.dma_start(w4_codes[first - 1][:], w4_words.bitcast(I32)[first - 1])
         nc.sync.dma_start(w4_codes[second - 1][:], w4_words.bitcast(I32)[second - 1])
         nc.sync.dma_start(w8_codes[:], w8_words[0].rearrange("p n i -> p (n i)").bitcast(I32))
-        nc.sync.dma_start(prev_sb[:], prev.rearrange("(m p) j -> p m j", p=P))
         for q in range(4):
             nc.sync.dma_start(w2_scales[32 * q : 32 * q + 4, 0, :], w8_rows[0, 4 * q : 4 * q + 4, :])
+        nc.sync.dma_start(prev_sb[:], prev.rearrange("(m p) j -> p m j", p=P))
 
         picked_words = []
         for a in range(2):
             words = keep.tile([P, S], U32, name=f"picked_words{a}", align_bytes=256)
             nc.vector.tensor_copy(words[:], table_words[a][:].bitcast(U32).indirect(offsets[:]))
             picked_words.append(words)
-        picked_scales = keep.tile([P, S], U8, name="picked_scales", align_bytes=256)
-        nc.vector.tensor_copy(picked_scales[:], table_scales[:].bitcast(U8).indirect(offsets[:]))
+        picked_scales = []
+        for a in range(2):
+            plane = keep.tile([P, S], U8, name=f"picked_scales{a}", align_bytes=256)
+            nc.vector.tensor_copy(plane[:], table_scales[:, a, :].bitcast(U8).indirect(offsets[:]))
+            picked_scales.append(plane)
 
         grouped, codes, scales = {}, {}, {}
         for b in range(3):
@@ -139,7 +145,7 @@ def tile_list_tabmlp_mix_res_kernel(
                     lhsT=codes[b, a][:, cols].bitcast(FP8),
                     lhsT_scale=scales[b, a][:, cols],
                     rhs=picked_words[a][:, toks].bitcast(FP8),
-                    rhs_scale=picked_scales[4 * a : P, toks],
+                    rhs_scale=picked_scales[a][:, toks],
                     start=(a, t) == steps[0],
                     stop=(a, t) == steps[-1],
                 )

@@ -67,7 +67,8 @@ def tile_list_tabmlp_mix_res_kernel(
         load_w1(first, 1, 0, 512)
         load_w1(second, 0, 0, 512)
         load_w1(second, 1, 0, 512)
-        load_w1(last, 0, 0, 512)
+        load_w1(last, 0, 0, 256)
+        load_w1(last, 0, 256, 512)
         load_w1(last, 1, 0, 256)
         load_w1(last, 1, 256, 384)
         load_w1(last, 1, 384, 512)
@@ -137,6 +138,8 @@ def tile_list_tabmlp_mix_res_kernel(
             passes = [(a, t, h) for a, t in steps for h in range(2)]
             if b == last:
                 passes = passes[:8] + passes[8::2] + passes[9::2]
+            if b == second:
+                passes = passes[0::2] + passes[1::2]
             for a, t, h in passes:
                 cols = slice(HALF * t, HALF * (t + 1))
                 toks = slice(HALF * h, HALF * (h + 1))
@@ -158,7 +161,7 @@ def tile_list_tabmlp_mix_res_kernel(
             shared = {
                 (first, 0): f"raw{second}0_0",
                 (first, 1): f"raw{second}1_0",
-                (second, 0): f"raw{last}1_0",
+                (second, 0): f"raw{last}0_256",
                 (second, 1): f"raw{last}1_384",
             }
             tile = keep.tile([P, HALF, 4], BF16, name=shared.get((b, h), f"h_grouped{h}"), align_bytes=256)
@@ -206,11 +209,12 @@ def tile_list_tabmlp_mix_res_kernel(
         hidden_matmuls(second, in_order[4:6] + in_order[0:4] + in_order[6:8])
         hidden_quantise(first, 0)
         hidden_quantise(first, 1)
-        split(last, 0, 0, 0, 128, 48)
+        split(last, 0, 0, 0, 64, 16)
+        split(last, 0, 256, 64, 128, 16)
         quantise(last, 0, 0, 0, 1024)
         quantise(last, 0, 1, 0, 1024)
-        split(last, 1, 0, 0, 64, 16)
         relu(nc.scalar, second, 0)
+        split(last, 1, 0, 0, 64, 16)
         split(last, 1, 256, 64, 96, 16)
         for t in range(2):
             quantise(last, 1, 0, 512 * t + 0, 512 * t + 256)

@@ -33,7 +33,7 @@ def tile_list_tabmlp_mix_res_kernel(
         table_scales = keep.tile([P, 2, T // 4], I32, name="table_scales", align_bytes=256)
         w2_scales = keep.tile([P, 3, M // 4], I32, name="w2_scales", align_bytes=256)
         w8_codes = keep.tile([P, M], I32, name="w8_codes", align_bytes=256)
-        w4_codes = [keep.tile([P, M // 2], I32, name=f"w4_codes{a}", align_bytes=256) for a in range(2)]
+        w4_codes = keep.tile([P, 2, M // 2], I32, name="w4_codes", align_bytes=256)
         prev_sb = keep.tile([P, 4, S], F32, name="prev_sb", align_bytes=256)
 
         nc.vector.memset(table_scales[:], 0)
@@ -76,12 +76,11 @@ def tile_list_tabmlp_mix_res_kernel(
             nc.sync.dma_start(
                 w2_scales[32 * q : 32 * q + 4, 1:3, :], w4_rows[:, 4 * q : 4 * q + 4, :].rearrange("a q c -> q a c")
             )
-        nc.sync.dma_start(w4_codes[first - 1][:], w4_words.bitcast(I32)[first - 1])
-        nc.sync.dma_start(w4_codes[second - 1][:], w4_words.bitcast(I32)[second - 1])
+        nc.sync.dma_start(w4_codes[:], w4_words.bitcast(I32).rearrange("a p c -> p a c"))
         nc.sync.dma_start(w8_codes[:], w8_words[0].rearrange("p n i -> p (n i)").bitcast(I32))
+        nc.sync.dma_start(prev_sb[:], prev.rearrange("(m p) j -> p m j", p=P))
         for q in range(4):
             nc.sync.dma_start(w2_scales[32 * q : 32 * q + 4, 0, :], w8_rows[0, 4 * q : 4 * q + 4, :])
-        nc.sync.dma_start(prev_sb[:], prev.rearrange("(m p) j -> p m j", p=P))
 
         picked_words = []
         for a in range(2):
@@ -132,6 +131,21 @@ def tile_list_tabmlp_mix_res_kernel(
 
         banks = {}
 
+        def warm_up():
+            idle = psum.tile([P, S], F32, name="hidden10")
+            moving = [(codes[last, 1][:, 0:64], scales[last, 1][:, 0:64])]
+            moving.extend([(picked_words[0][:], picked_scales[0][:])] * 3)
+            for words, plane in moving:
+                nc.tensor.matmul_mx(
+                    out=idle[:, 0 : words.shape[1]],
+                    lhsT=codes[last, 0][:, 0:HALF].bitcast(FP8),
+                    lhsT_scale=scales[last, 0][:, 0:HALF],
+                    rhs=words.bitcast(FP8),
+                    rhs_scale=plane,
+                    start=True,
+                    stop=True,
+                )
+
         def hidden_matmuls(b, steps):
             for h in range(2):
                 banks[b, h] = psum.tile([P, 4, HALF], F32, name=f"hidden{int(b == second)}{h}")
@@ -140,7 +154,9 @@ def tile_list_tabmlp_mix_res_kernel(
                 passes = passes[:8] + passes[8::2] + passes[9::2]
             if b == second:
                 passes = passes[0::2] + passes[1::2]
-            for a, t, h in passes:
+            for i, (a, t, h) in enumerate(passes):
+                if b == last and i == 8:
+                    warm_up()
                 cols = slice(HALF * t, HALF * (t + 1))
                 toks = slice(HALF * h, HALF * (h + 1))
                 nc.tensor.matmul_mx(
@@ -187,7 +203,7 @@ def tile_list_tabmlp_mix_res_kernel(
             if b == 0:
                 lhsT = w8_codes[:, HALF * m : HALF * (m + 1)].bitcast(FP8)
             else:
-                lhsT = w4_codes[b - 1][:, 64 * m : 64 * (m + 1)].bitcast(FP4)
+                lhsT = w4_codes[:, b - 1, 64 * m : 64 * (m + 1)].bitcast(FP4)
             nc.tensor.matmul_mx(
                 out=outs[m, toks.start // HALF] if toks.stop - toks.start == HALF else whole[m - 1][:],
                 lhsT=lhsT,

@@ -131,21 +131,6 @@ def tile_list_tabmlp_mix_res_kernel(
 
         banks = {}
 
-        def warm_up():
-            idle = psum.tile([P, S], F32, name="hidden10")
-            moving = [(codes[last, 1][:, 0:64], scales[last, 1][:, 0:64])]
-            moving.extend([(picked_words[0][:], picked_scales[0][:])] * 3)
-            for words, plane in moving:
-                nc.tensor.matmul_mx(
-                    out=idle[:, 0 : words.shape[1]],
-                    lhsT=codes[last, 0][:, 0:HALF].bitcast(FP8),
-                    lhsT_scale=scales[last, 0][:, 0:HALF],
-                    rhs=words.bitcast(FP8),
-                    rhs_scale=plane,
-                    start=True,
-                    stop=True,
-                )
-
         def hidden_matmuls(b, steps):
             for h in range(2):
                 banks[b, h] = psum.tile([P, 4, HALF], F32, name=f"hidden{int(b == second)}{h}")
@@ -154,9 +139,7 @@ def tile_list_tabmlp_mix_res_kernel(
                 passes = passes[:8] + passes[8::2] + passes[9::2]
             if b == second:
                 passes = passes[0::2] + passes[1::2]
-            for i, (a, t, h) in enumerate(passes):
-                if b == last and i == 8:
-                    warm_up()
+            for a, t, h in passes:
                 cols = slice(HALF * t, HALF * (t + 1))
                 toks = slice(HALF * h, HALF * (h + 1))
                 nc.tensor.matmul_mx(

@@ -29,12 +29,12 @@ def tile_list_tabmlp_mix_res_kernel(
         psum = ctx.enter_context(tc.psum_pool(name="psum", bufs=1))
 
         offsets = keep.tile([P, S // 16], U16, name="offsets")
-        table_words = [keep.tile([P, T], I32, name=f"table_words{a}", align_bytes=256) for a in range(2)]
+        table_words = keep.tile([P, 2, T], I32, name="table_words", align_bytes=256)
         table_scales = keep.tile([P, 2, T // 4], I32, name="table_scales", align_bytes=256)
         w2_scales = keep.tile([P, 3, M // 4], I32, name="w2_scales", align_bytes=256)
         w8_codes = keep.tile([P, M], I32, name="w8_codes", align_bytes=256)
         w4_codes = keep.tile([P, 2, M // 2], I32, name="w4_codes", align_bytes=256)
-        prev_sb = keep.tile([P, 4, S], F32, name="prev_sb", align_bytes=256)
+        prev_sb = [keep.tile([P, 2, S], F32, name=f"prev_sb{i}", align_bytes=256) for i in range(2)]
 
         nc.vector.memset(table_scales[:], 0)
         nc.vector.memset(w2_scales[:], 0)
@@ -53,10 +53,7 @@ def tile_list_tabmlp_mix_res_kernel(
         w8_rows = w8_scales.bitcast(I32)
         w4_rows = w4_scales.bitcast(I32)
 
-        for a in range(2):
-            nc.sync.dma_start(
-                table_words[a][:], tab_i32[a, 0 : WORD_BYTES // 4].rearrange("(p c) -> p c", p=P)
-            )
+        nc.sync.dma_start(table_words[:], tab_i32[:, 0 : WORD_BYTES // 4].rearrange("a (p c) -> p a c", p=P))
         nc.sync.dma_start(offsets[:], offs)
         load_w1(first, 0, 0, 512)
         for q in range(4):
@@ -78,14 +75,15 @@ def tile_list_tabmlp_mix_res_kernel(
             )
         nc.sync.dma_start(w4_codes[:], w4_words.bitcast(I32).rearrange("a p c -> p a c"))
         nc.sync.dma_start(w8_codes[:], w8_words[0].rearrange("p n i -> p (n i)").bitcast(I32))
-        nc.sync.dma_start(prev_sb[:], prev.rearrange("(m p) j -> p m j", p=P))
+        nc.sync.dma_start(prev_sb[0][:], prev[0:256, :].rearrange("(m p) j -> p m j", p=P))
         for q in range(4):
             nc.sync.dma_start(w2_scales[32 * q : 32 * q + 4, 0, :], w8_rows[0, 4 * q : 4 * q + 4, :])
+        nc.sync.dma_start(prev_sb[1][:], prev[256:512, :].rearrange("(m p) j -> p m j", p=P))
 
         picked_words = []
         for a in range(2):
             words = keep.tile([P, S], U32, name=f"picked_words{a}", align_bytes=256)
-            nc.vector.tensor_copy(words[:], table_words[a][:].bitcast(U32).indirect(offsets[:]))
+            nc.vector.tensor_copy(words[:], table_words[:, a, :].bitcast(U32).indirect(offsets[:]))
             picked_words.append(words)
         picked_scales = []
         for a in range(2):
@@ -227,30 +225,42 @@ def tile_list_tabmlp_mix_res_kernel(
         relu(nc.scalar, second, 1)
         hidden_matmuls(last, in_order)
         hidden_quantise(second, 0)
+        relu(nc.vector, last, 0)
         hidden_quantise(second, 1)
+        relu(nc.scalar, last, 1)
 
+        halves = [slice(0, HALF), slice(HALF, S)]
         whole = [psum.tile([P, S], F32, name=f"out{m}") for m in range(1, 4)]
-        outs = {(m, h): whole[m - 1][:, HALF * h : HALF * (h + 1)] for m in range(1, 4) for h in range(2)}
+        outs = {(m, h): whole[m - 1][:, halves[h]] for m in range(1, 4) for h in range(2)}
         outs[0, 0] = psum.tile([P, HALF], F32, name="out0")[:]
         outs[0, 1] = psum.tile([P, HALF], F32, name="hidden10")[:]
-        halves = [slice(0, HALF), slice(HALF, S)]
-        for b, h in ((first, 0), (second, 0), (second, 1), (first, 1)):
-            for m in range(4):
-                out_matmul(m, halves[h], b, (b, h) == (first, 0) or (m, b, h) == (0, second, 1), False)
-        relu(nc.scalar, last, 0)
-        relu(nc.vector, last, 1)
+
+        def finish(m, toks, queue):
+            n = toks.stop - toks.start
+            result = keep.tile([P, n], F32, name=f"result{m}_{toks.start}", align_bytes=256)
+            total = outs[m, toks.start // HALF] if n == HALF else whole[m - 1][:]
+            nc.vector.tensor_add(result[:], total, prev_sb[m // 2][:, m % 2, toks])
+            queue.dma_start(out[P * m : P * (m + 1), toks], result[:])
+
+        for m in range(4):
+            out_matmul(m, halves[0], second, True, False)
+            out_matmul(m, halves[0], first, False, False)
+            if m:
+                out_matmul(m, halves[1], first, False, False)
+        for m in (1, 2):
+            out_matmul(m, halves[1], second, False, False)
         for h in range(2):
             hidden_quantise(last, h)
-        for h in range(2):
-            out_matmul(0, halves[h], last, False, True)
-        for m in range(1, 4):
+        out_matmul(0, halves[0], last, False, True)
+        for m in (1, 2):
             out_matmul(m, slice(0, S), last, False, True)
-        for h in range(2):
-            part = keep.tile([P, HALF], F32, name=f"part{h}", align_bytes=256)
-            nc.vector.tensor_add(part[:], outs[0, h], prev_sb[:, 0, halves[h]])
-            nc.sync.dma_start(out[0:P, halves[h]], part[:])
-        for m in range(1, 4):
-            result = keep.tile([P, S], F32, name=f"result{m}", align_bytes=256)
-            nc.vector.tensor_add(result[:], whole[m - 1][:], prev_sb[:, m, :])
-            queue = nc.scalar if m % 2 == 1 else nc.sync
-            queue.dma_start(out[P * m : P * (m + 1), :], result[:])
+        out_matmul(3, halves[1], second, False, False)
+        out_matmul(3, slice(0, S), last, False, True)
+        out_matmul(0, halves[1], second, True, False)
+        out_matmul(0, halves[1], first, False, False)
+        out_matmul(0, halves[1], last, False, True)
+        finish(0, halves[0], nc.sync)
+        finish(1, slice(0, S), nc.scalar)
+        finish(2, slice(0, S), nc.sync)
+        finish(3, slice(0, S), nc.scalar)
+        finish(0, halves[1], nc.sync)

@@ -5,9 +5,15 @@ import concourse.mybir as mybir
 FLOPS = 1207959552
 
 P = 128
-K, H, M, T, S = 1024, 1536, 512, 512, 256
+PASS = 512
+M, T, S = 512, 512, 256
 HALF = 128
 WORD_BYTES = 512 * T
+ALIGN = 256
+
+FIRST, SECOND, LAST = 1, 2, 0
+
+EXTRA_WHOLE, EXTRA_HALF, EXTRA_FOURTH = 32, 16, 16
 
 F32 = mybir.dt.float32
 BF16 = mybir.dt.bfloat16
@@ -29,22 +35,21 @@ def tile_list_tabmlp_mix_res_kernel(
         psum = ctx.enter_context(tc.psum_pool(name="psum", bufs=1))
 
         offsets = keep.tile([P, S // 16], U16, name="offsets")
-        table_words = keep.tile([P, 2, T], I32, name="table_words", align_bytes=256)
-        table_scales = keep.tile([P, 2, T // 4], I32, name="table_scales", align_bytes=256)
-        w2_scales = keep.tile([P, 3, M // 4], I32, name="w2_scales", align_bytes=256)
-        w8_codes = keep.tile([P, M], I32, name="w8_codes", align_bytes=256)
-        w4_codes = keep.tile([P, 2, M // 2], I32, name="w4_codes", align_bytes=256)
-        prev_sb = [keep.tile([P, 2, S], F32, name=f"prev_sb{i}", align_bytes=256) for i in range(2)]
+        table_words = keep.tile([P, 2, T], I32, name="table_words", align_bytes=ALIGN)
+        table_scales = keep.tile([P, 2, T // 4], I32, name="table_scales", align_bytes=ALIGN)
+        w2_scales = keep.tile([P, 3, M // 4], I32, name="w2_scales", align_bytes=ALIGN)
+        w8_codes = keep.tile([P, M], I32, name="w8_codes", align_bytes=ALIGN)
+        w4_codes = keep.tile([P, 2, M // 2], I32, name="w4_codes", align_bytes=ALIGN)
+        prev_sb = [keep.tile([P, 2, S], F32, name=f"prev_sb{i}", align_bytes=ALIGN) for i in range(2)]
 
         nc.vector.memset(table_scales[:], 0)
         nc.vector.memset(w2_scales[:], 0)
 
         raws = {}
-        first, second, last = 1, 2, 0
 
         def load_w1(b, a, c0, c1):
-            raw = keep.tile([P, 4, c1 - c0], F32, name=f"raw{b}{a}_{c0}", align_bytes=256)
-            rows = w1[512 * a : 512 * (a + 1), 512 * b + c0 : 512 * b + c1]
+            raw = keep.tile([P, 4, c1 - c0], F32, name=f"raw{b}{a}_{c0}", align_bytes=ALIGN)
+            rows = w1[PASS * a : PASS * (a + 1), PASS * b + c0 : PASS * b + c1]
             nc.sync.dma_start(raw[:], rows.rearrange("(p j) c -> p j c", j=4))
             raws[b, a, c0] = raw
 
@@ -55,212 +60,222 @@ def tile_list_tabmlp_mix_res_kernel(
 
         nc.sync.dma_start(table_words[:], tab_i32[:, 0 : WORD_BYTES // 4].rearrange("a (p c) -> p a c", p=P))
         nc.sync.dma_start(offsets[:], offs)
-        load_w1(first, 0, 0, 512)
-        for q in range(4):
+        load_w1(FIRST, 0, 0, PASS)
+        for quad in range(4):
             nc.sync.dma_start(
-                table_scales[32 * q : 32 * q + 4],
-                tab_scale_rows[:, 4 * q : 4 * q + 4, :].rearrange("a q c -> q a c"),
+                table_scales[32 * quad : 32 * quad + 4],
+                tab_scale_rows[:, 4 * quad : 4 * quad + 4, :].rearrange("a q c -> q a c"),
             )
-        load_w1(first, 1, 0, 512)
-        load_w1(second, 0, 0, 512)
-        load_w1(second, 1, 0, 512)
-        load_w1(last, 0, 0, 256)
-        load_w1(last, 0, 256, 512)
-        load_w1(last, 1, 0, 256)
-        load_w1(last, 1, 256, 384)
-        load_w1(last, 1, 384, 512)
-        for q in range(4):
+        load_w1(FIRST, 1, 0, PASS)
+        load_w1(SECOND, 0, 0, PASS)
+        load_w1(SECOND, 1, 0, PASS)
+        load_w1(LAST, 0, 0, 256)
+        load_w1(LAST, 0, 256, 512)
+        load_w1(LAST, 1, 0, 256)
+        load_w1(LAST, 1, 256, 384)
+        load_w1(LAST, 1, 384, 512)
+        for quad in range(4):
             nc.sync.dma_start(
-                w2_scales[32 * q : 32 * q + 4, 1:3, :], w4_rows[:, 4 * q : 4 * q + 4, :].rearrange("a q c -> q a c")
+                w2_scales[32 * quad : 32 * quad + 4, 1:3, :],
+                w4_rows[:, 4 * quad : 4 * quad + 4, :].rearrange("a q c -> q a c"),
             )
         nc.sync.dma_start(w4_codes[:], w4_words.bitcast(I32).rearrange("a p c -> p a c"))
         nc.sync.dma_start(w8_codes[:], w8_words[0].rearrange("p n i -> p (n i)").bitcast(I32))
         nc.sync.dma_start(prev_sb[0][:], prev[0:256, :].rearrange("(m p) j -> p m j", p=P))
-        for q in range(4):
-            nc.sync.dma_start(w2_scales[32 * q : 32 * q + 4, 0, :], w8_rows[0, 4 * q : 4 * q + 4, :])
+        for quad in range(4):
+            nc.sync.dma_start(w2_scales[32 * quad : 32 * quad + 4, 0, :], w8_rows[0, 4 * quad : 4 * quad + 4, :])
         nc.sync.dma_start(prev_sb[1][:], prev[256:512, :].rearrange("(m p) j -> p m j", p=P))
 
         picked_words = []
         for a in range(2):
-            words = keep.tile([P, S], U32, name=f"picked_words{a}", align_bytes=256)
+            words = keep.tile([P, S], U32, name=f"picked_words{a}", align_bytes=ALIGN)
             nc.vector.tensor_copy(words[:], table_words[:, a, :].bitcast(U32).indirect(offsets[:]))
             picked_words.append(words)
         picked_scales = []
         for a in range(2):
-            plane = keep.tile([P, S], U8, name=f"picked_scales{a}", align_bytes=256)
-            nc.vector.tensor_copy(plane[:], table_scales[:, a, :].bitcast(U8).indirect(offsets[:]))
-            picked_scales.append(plane)
+            scale_bytes = keep.tile([P, S], U8, name=f"picked_scales{a}", align_bytes=ALIGN)
+            nc.vector.tensor_copy(scale_bytes[:], table_scales[:, a, :].bitcast(U8).indirect(offsets[:]))
+            picked_scales.append(scale_bytes)
 
         grouped, codes, scales = {}, {}, {}
         for b in range(3):
             for a in range(2):
                 for u in range(2):
-                    grouped[b, a, u] = keep.tile([P, 1024], BF16, name=f"grouped{b}{a}{u}", align_bytes=256)
-                codes[b, a] = keep.tile([P, 512], U32, name=f"w1_codes{b}{a}", align_bytes=256)
-                scales[b, a] = keep.tile([P, 512], U8, name=f"w1_scales{b}{a}", align_bytes=256)
+                    grouped[b, a, u] = keep.tile([P, 1024], BF16, name=f"grouped{b}{a}{u}", align_bytes=ALIGN)
+                codes[b, a] = keep.tile([P, PASS], U32, name=f"w1_codes{b}{a}", align_bytes=ALIGN)
+                scales[b, a] = keep.tile([P, PASS], U8, name=f"w1_scales{b}{a}", align_bytes=ALIGN)
 
         def interleave(engine, b, a, c0, u, m0, m1):
-            view = grouped[b, a, u][:].rearrange("p (t m j) -> p m j t", t=2, j=4)
+            dst = grouped[b, a, u][:].rearrange("p (t m j) -> p m j t", t=2, j=4)[:, m0:m1]
             src = raws[b, a, c0][:].rearrange("p j (m t) -> p m j t", t=4)
-            dst = view[:, m0:m1]
             src = src[:, m0 - c0 // 4 : m1 - c0 // 4, :, 2 * u : 2 * u + 2]
             if engine is nc.scalar:
                 nc.scalar.copy(dst, src)
             else:
                 nc.vector.tensor_copy(dst, src)
 
+        def share_copies(b, a, c0, c1, extra):
+            m0, m1 = c0 // 4, c1 // 4
+            interleave(nc.scalar, b, a, c0, 1, m0 + extra, m1)
+            interleave(nc.vector, b, a, c0, 0, m0, m1)
+            if extra:
+                interleave(nc.vector, b, a, c0, 1, m0, m0 + extra)
+
         def quantise(b, a, u, i0, i1):
-            o = slice(256 * u + i0 // 4, 256 * u + i1 // 4)
+            cols = slice(256 * u + i0 // 4, 256 * u + i1 // 4)
             nc.vector.quantize_mx(
-                out=codes[b, a][:, o].bitcast(FP8), scales=scales[b, a][:, o], in_=grouped[b, a, u][:, i0:i1]
+                out=codes[b, a][:, cols].bitcast(FP8), scales=scales[b, a][:, cols], in_=grouped[b, a, u][:, i0:i1]
             )
 
-        def split(b, a, c0, m0, m1, cut):
-            if m0 + cut < m1:
-                interleave(nc.scalar, b, a, c0, 1, m0 + cut, m1)
-            interleave(nc.vector, b, a, c0, 0, m0, m1)
-            if cut:
-                interleave(nc.vector, b, a, c0, 1, m0, m0 + cut)
+        def quantise_part(b, a):
+            for u in range(2):
+                quantise(b, a, u, 0, 1024)
 
-        def whole_block(b, a):
-            split(b, a, 0, 0, 128, 32)
-            quantise(b, a, 0, 0, 1024)
-            quantise(b, a, 1, 0, 1024)
+        def quantise_half_slices(u, upper):
+            for t in range(2):
+                quantise(LAST, 1, u, 512 * t + 256 * upper, 512 * t + 256 * (upper + 1))
 
         banks = {}
+        in_order = [(a, t) for a in range(2) for t in range(4)]
 
-        def hidden_matmuls(b, steps):
+        def hidden_matmuls(b, passes):
             for h in range(2):
-                banks[b, h] = psum.tile([P, 4, HALF], F32, name=f"hidden{int(b == second)}{h}")
-            passes = [(a, t, h) for a, t in steps for h in range(2)]
-            if b == last:
-                passes = passes[:8] + passes[8::2] + passes[9::2]
-            if b == second:
-                passes = passes[0::2] + passes[1::2]
+                banks[b, h] = psum.tile([P, 4, HALF], F32, name=f"hidden{int(b == SECOND)}{h}")
             for a, t, h in passes:
                 cols = slice(HALF * t, HALF * (t + 1))
                 toks = slice(HALF * h, HALF * (h + 1))
+                of_bank = [step for step in passes if step[2] == h]
                 nc.tensor.matmul_mx(
                     out=banks[b, h][:, t, :],
                     lhsT=codes[b, a][:, cols].bitcast(FP8),
                     lhsT_scale=scales[b, a][:, cols],
                     rhs=picked_words[a][:, toks].bitcast(FP8),
                     rhs_scale=picked_scales[a][:, toks],
-                    start=(a, t) == steps[0],
-                    stop=(a, t) == steps[-1],
+                    start=(a, t, h) == of_bank[0],
+                    stop=(a, t, h) == of_bank[-1],
                 )
+
+        early_first_bank = [(0, t, h) for t in range(4) for h in range(2)]
+        early_first_bank.extend((1, t, h) for h in range(2) for t in range(4))
+        one_stretch = [(a, t, h) for h in range(2) for a, t in in_order[4:6] + in_order[0:4] + in_order[6:8]]
 
         h_grouped, h_codes, h_scales = {}, {}, {}
         for b in range(3):
-            h_scales[b] = keep.tile([P, S], U8, name=f"h_scales{b}", align_bytes=256)
+            h_scales[b] = keep.tile([P, S], U8, name=f"h_scales{b}", align_bytes=ALIGN)
 
-        def relu(engine, b, h):
-            shared = {
-                (first, 0): f"raw{second}0_0",
-                (first, 1): f"raw{second}1_0",
-                (second, 0): f"raw{last}0_256",
-                (second, 1): f"raw{last}1_384",
-            }
-            tile = keep.tile([P, HALF, 4], BF16, name=shared.get((b, h), f"h_grouped{h}"), align_bytes=256)
-            h_grouped[b, h] = tile[:]
+        def relu(engine, b, h, dst):
+            h_grouped[b, h] = dst
             src = banks[b, h][:].rearrange("p t n -> p n t")
             if engine is nc.scalar:
-                nc.scalar.activation(h_grouped[b, h], src, RELU)
+                nc.scalar.activation(dst, src, RELU)
             else:
-                nc.vector.tensor_scalar_max(h_grouped[b, h], src, 0.0)
+                nc.vector.tensor_scalar_max(dst, src, 0.0)
 
-        def hidden_quantise(b, h):
-            if h == 0:
-                name = {first: f"grouped{second}11", second: f"grouped{last}11", last: "h_codes_last"}[b]
-                h_codes[b] = keep.tile([P, S], U32, name=name, align_bytes=256)
-            toks = slice(HALF * h, HALF * (h + 1))
+        def relu_tile(tag):
+            tile = keep.tile([P, HALF, 4], BF16, name=tag, align_bytes=ALIGN)
+            return tile[:]
+
+        def codes_tile(tag, width):
+            tile = keep.tile([P, width], U32, name=tag, align_bytes=ALIGN)
+            return tile[:]
+
+        def hidden_quantise(b, h, dst):
+            h_codes[b, h] = dst
             nc.vector.quantize_mx(
-                out=h_codes[b][:, toks].bitcast(FP8),
-                scales=h_scales[b][:, toks],
+                out=dst.bitcast(FP8),
+                scales=h_scales[b][:, HALF * h : HALF * (h + 1)],
                 in_=h_grouped[b, h].rearrange("p n t -> p (n t)"),
             )
 
-        def out_matmul(m, toks, b, start, stop):
+        halves = [slice(0, HALF), slice(HALF, S)]
+        both_halves = slice(0, S)
+
+        for a in range(2):
+            share_copies(FIRST, a, 0, PASS, EXTRA_WHOLE)
+            quantise_part(FIRST, a)
+        hidden_matmuls(FIRST, early_first_bank)
+        share_copies(SECOND, 0, 0, PASS, EXTRA_WHOLE)
+        quantise_part(SECOND, 0)
+        first_h = keep.tile([P, 2, HALF, 4], BF16, name=f"raw{SECOND}0_0", align_bytes=ALIGN)
+        for h in range(2):
+            relu(nc.scalar, FIRST, h, first_h[:, h])
+        hidden_quantise(FIRST, 0, codes_tile(f"grouped{SECOND}01", HALF))
+        share_copies(SECOND, 1, 0, PASS, EXTRA_FOURTH)
+        quantise_part(SECOND, 1)
+        hidden_quantise(FIRST, 1, codes_tile(f"raw{SECOND}1_0", HALF))
+        hidden_matmuls(SECOND, one_stretch)
+
+        share_copies(LAST, 0, 0, 256, 0)
+        share_copies(LAST, 0, 256, 512, EXTRA_HALF)
+        quantise_part(LAST, 0)
+        relu(nc.scalar, SECOND, 0, relu_tile(f"raw{LAST}0_256"))
+        share_copies(LAST, 1, 0, 256, EXTRA_HALF)
+        share_copies(LAST, 1, 256, 384, 0)
+        quantise_half_slices(0, 0)
+        share_copies(LAST, 1, 384, 512, 0)
+        quantise_half_slices(1, 0)
+        quantise_half_slices(0, 1)
+        quantise_half_slices(1, 1)
+        relu(nc.scalar, SECOND, 1, relu_tile(f"raw{LAST}1_384"))
+        hidden_matmuls(LAST, early_first_bank)
+        second_h = codes_tile(f"grouped{LAST}11", S)
+        hidden_quantise(SECOND, 0, second_h[:, halves[0]])
+        relu(nc.vector, LAST, 0, relu_tile("h_grouped0"))
+        hidden_quantise(SECOND, 1, second_h[:, halves[1]])
+        relu(nc.scalar, LAST, 1, relu_tile("h_grouped1"))
+
+        whole = {m: psum.tile([P, S], F32, name=f"out{m}") for m in range(1, 4)}
+        sums = {(m, h): whole[m][:, halves[h]] for m in range(1, 4) for h in range(2)}
+        sums[0, 0] = psum.tile([P, HALF], F32, name="out0")[:]
+        sums[0, 1] = psum.tile([P, HALF], F32, name="hidden10")[:]
+
+        def out_matmul(dst, m, b, moving, toks, start, stop):
             if b == 0:
-                lhsT = w8_codes[:, HALF * m : HALF * (m + 1)].bitcast(FP8)
+                weights = w8_codes[:, HALF * m : HALF * (m + 1)].bitcast(FP8)
             else:
-                lhsT = w4_codes[:, b - 1, 64 * m : 64 * (m + 1)].bitcast(FP4)
+                weights = w4_codes[:, b - 1, 64 * m : 64 * (m + 1)].bitcast(FP4)
             nc.tensor.matmul_mx(
-                out=outs[m, toks.start // HALF] if toks.stop - toks.start == HALF else whole[m - 1][:],
-                lhsT=lhsT,
+                out=dst,
+                lhsT=weights,
                 lhsT_scale=w2_scales[:, b, 32 * m : 32 * (m + 1)].bitcast(U8),
-                rhs=h_codes[b][:, toks].bitcast(FP8),
+                rhs=moving.bitcast(FP8),
                 rhs_scale=h_scales[b][:, toks],
                 start=start,
                 stop=stop,
             )
 
-        in_order = [(a, t) for a in range(2) for t in range(4)]
-        whole_block(first, 0)
-        whole_block(first, 1)
-        hidden_matmuls(first, in_order)
-        whole_block(second, 0)
-        relu(nc.scalar, first, 0)
-        whole_block(second, 1)
-        relu(nc.scalar, first, 1)
-        hidden_matmuls(second, in_order[4:6] + in_order[0:4] + in_order[6:8])
-        hidden_quantise(first, 0)
-        hidden_quantise(first, 1)
-        split(last, 0, 0, 0, 64, 16)
-        split(last, 0, 256, 64, 128, 16)
-        quantise(last, 0, 0, 0, 1024)
-        quantise(last, 0, 1, 0, 1024)
-        relu(nc.scalar, second, 0)
-        split(last, 1, 0, 0, 64, 16)
-        split(last, 1, 256, 64, 96, 16)
-        for t in range(2):
-            quantise(last, 1, 0, 512 * t + 0, 512 * t + 256)
-        split(last, 1, 384, 96, 128, 0)
-        for t in range(2):
-            quantise(last, 1, 1, 512 * t + 0, 512 * t + 256)
-        for t in range(2):
-            quantise(last, 1, 0, 512 * t + 256, 512 * t + 512)
-        for t in range(2):
-            quantise(last, 1, 1, 512 * t + 256, 512 * t + 512)
-        relu(nc.scalar, second, 1)
-        hidden_matmuls(last, in_order)
-        hidden_quantise(second, 0)
-        relu(nc.vector, last, 0)
-        hidden_quantise(second, 1)
-        relu(nc.scalar, last, 1)
+        def half_pass(m, h, b, start=False, stop=False):
+            out_matmul(sums[m, h], m, b, h_codes[b, h], halves[h], start, stop)
 
-        halves = [slice(0, HALF), slice(HALF, S)]
-        whole = [psum.tile([P, S], F32, name=f"out{m}") for m in range(1, 4)]
-        outs = {(m, h): whole[m - 1][:, halves[h]] for m in range(1, 4) for h in range(2)}
-        outs[0, 0] = psum.tile([P, HALF], F32, name="out0")[:]
-        outs[0, 1] = psum.tile([P, HALF], F32, name="hidden10")[:]
+        def closing_pass(m):
+            out_matmul(whole[m][:], m, LAST, last_h, both_halves, False, True)
 
-        def finish(m, toks, queue):
-            n = toks.stop - toks.start
-            result = keep.tile([P, n], F32, name=f"result{m}_{toks.start}", align_bytes=256)
-            total = outs[m, toks.start // HALF] if n == HALF else whole[m - 1][:]
+        def finish(total, m, toks, queue):
+            width = toks.stop - toks.start
+            result = keep.tile([P, width], F32, name=f"result{m}_{toks.start}", align_bytes=ALIGN)
             nc.vector.tensor_add(result[:], total, prev_sb[m // 2][:, m % 2, toks])
             queue.dma_start(out[P * m : P * (m + 1), toks], result[:])
 
         for m in range(4):
-            out_matmul(m, halves[0], second, True, False)
-            out_matmul(m, halves[0], first, False, False)
-            if m:
-                out_matmul(m, halves[1], first, False, False)
+            half_pass(m, 0, SECOND, start=True)
+            half_pass(m, 0, FIRST)
+            if m > 0:
+                half_pass(m, 1, FIRST)
         for m in (1, 2):
-            out_matmul(m, halves[1], second, False, False)
+            half_pass(m, 1, SECOND)
+        last_h = codes_tile("h_codes_last", S)
         for h in range(2):
-            hidden_quantise(last, h)
-        out_matmul(0, halves[0], last, False, True)
+            hidden_quantise(LAST, h, last_h[:, halves[h]])
+        half_pass(0, 0, LAST, stop=True)
         for m in (1, 2):
-            out_matmul(m, slice(0, S), last, False, True)
-        out_matmul(3, halves[1], second, False, False)
-        out_matmul(3, slice(0, S), last, False, True)
-        out_matmul(0, halves[1], second, True, False)
-        out_matmul(0, halves[1], first, False, False)
-        out_matmul(0, halves[1], last, False, True)
-        finish(0, halves[0], nc.sync)
-        finish(1, slice(0, S), nc.scalar)
-        finish(2, slice(0, S), nc.sync)
-        finish(3, slice(0, S), nc.scalar)
-        finish(0, halves[1], nc.sync)
+            closing_pass(m)
+        half_pass(3, 1, SECOND)
+        closing_pass(3)
+        half_pass(0, 1, SECOND, start=True)
+        half_pass(0, 1, FIRST)
+        half_pass(0, 1, LAST, stop=True)
+
+        finish(sums[0, 0], 0, halves[0], nc.sync)
+        for m, queue in ((1, nc.scalar), (2, nc.sync), (3, nc.scalar)):
+            finish(whole[m][:], m, both_halves, queue)
+        finish(sums[0, 1], 0, halves[1], nc.sync)

@@ -53,6 +53,11 @@ def tile_list_tabmlp_mix_res_kernel(
             nc.sync.dma_start(raw[:], rows.rearrange("(p j) c -> p j c", j=4))
             raws[b, a, c0] = raw
 
+        def load_scale_rows(tile, planes, rows):
+            by_r = rows.rearrange("a (q r) c -> r q a c", r=4)
+            for r in range(4):
+                nc.sync.dma_start(tile[r:P:32, planes, :], by_r[r])
+
         tab_i32 = tab.bitcast(I32)
         tab_scale_rows = tab_i32[:, WORD_BYTES // 4 :].rearrange("a (q c) -> a q c", q=16)
         w8_rows = w8_scales.bitcast(I32)
@@ -61,11 +66,7 @@ def tile_list_tabmlp_mix_res_kernel(
         nc.sync.dma_start(table_words[:], tab_i32[:, 0 : WORD_BYTES // 4].rearrange("a (p c) -> p a c", p=P))
         nc.sync.dma_start(offsets[:], offs)
         load_w1(FIRST, 0, 0, PASS)
-        for quad in range(4):
-            nc.sync.dma_start(
-                table_scales[32 * quad : 32 * quad + 4],
-                tab_scale_rows[:, 4 * quad : 4 * quad + 4, :].rearrange("a q c -> q a c"),
-            )
+        load_scale_rows(table_scales, slice(0, 2), tab_scale_rows)
         load_w1(FIRST, 1, 0, PASS)
         load_w1(SECOND, 0, 0, PASS)
         load_w1(SECOND, 1, 0, PASS)
@@ -74,16 +75,11 @@ def tile_list_tabmlp_mix_res_kernel(
         load_w1(LAST, 1, 0, 256)
         load_w1(LAST, 1, 256, 384)
         load_w1(LAST, 1, 384, 512)
-        for quad in range(4):
-            nc.sync.dma_start(
-                w2_scales[32 * quad : 32 * quad + 4, 1:3, :],
-                w4_rows[:, 4 * quad : 4 * quad + 4, :].rearrange("a q c -> q a c"),
-            )
+        load_scale_rows(w2_scales, slice(1, 3), w4_rows)
         nc.sync.dma_start(w4_codes[:], w4_words.bitcast(I32).rearrange("a p c -> p a c"))
         nc.sync.dma_start(w8_codes[:], w8_words[0].rearrange("p n i -> p (n i)").bitcast(I32))
         nc.sync.dma_start(prev_sb[0][:], prev[0:256, :].rearrange("(m p) j -> p m j", p=P))
-        for quad in range(4):
-            nc.sync.dma_start(w2_scales[32 * quad : 32 * quad + 4, 0, :], w8_rows[0, 4 * quad : 4 * quad + 4, :])
+        load_scale_rows(w2_scales, slice(0, 1), w8_rows)
         nc.sync.dma_start(prev_sb[1][:], prev[256:512, :].rearrange("(m p) j -> p m j", p=P))
 
         picked_words = []

@@ -12,7 +12,6 @@ WORD_BYTES = 512 * T
 ALIGN = 256
 
 FIRST, SECOND, LAST = 1, 2, 0
-
 EXTRA_WHOLE, EXTRA_HALF, EXTRA_FOURTH = 32, 16, 16
 
 F32 = mybir.dt.float32
@@ -32,74 +31,82 @@ def tile_list_tabmlp_mix_res_kernel(
     nc = tc.nc
     with ExitStack() as ctx:
         keep = ctx.enter_context(tc.tile_pool(name="keep", bufs=1))
+        last = ctx.enter_context(tc.tile_pool(name="last", bufs=1))
+        rows_pool = ctx.enter_context(tc.tile_pool(name="rows", bufs=1))
         psum = ctx.enter_context(tc.psum_pool(name="psum", bufs=1))
 
-        offsets = keep.tile([P, S // 16], U16, name="offsets")
-        table_words = keep.tile([P, 2, T], I32, name="table_words", align_bytes=ALIGN)
-        table_scales = keep.tile([P, 2, T // 4], I32, name="table_scales", align_bytes=ALIGN)
-        w2_scales = keep.tile([P, 3, M // 4], I32, name="w2_scales", align_bytes=ALIGN)
-        w8_codes = keep.tile([P, M], I32, name="w8_codes", align_bytes=ALIGN)
-        w4_codes = keep.tile([P, 2, M // 2], I32, name="w4_codes", align_bytes=ALIGN)
-        prev_sb = [keep.tile([P, 2, S], F32, name=f"prev_sb{i}", align_bytes=ALIGN) for i in range(2)]
+        def sbuf(shape, dtype, name):
+            return keep.tile(shape, dtype, name=name, align_bytes=ALIGN)
 
-        nc.vector.memset(table_scales[:], 0)
-        nc.vector.memset(w2_scales[:], 0)
+        offsets = keep.tile([P, S // 16], U16, name="offsets")
+        table_words = sbuf([P, 2, T], I32, "table_words")
+        table_scales = sbuf([P, 4, T // 4], I32, "table_scales")
+        w4_planes = sbuf([P, 2, 2, M // 4], I32, "w4_planes")
+        w8_plane = sbuf([P, M // 4], I32, "w8_plane")
+        w8_rows = rows_pool.tile([4, 4, M // 4], I32, name="w8_rows", align_bytes=ALIGN, offset=0)
+        w8_codes = sbuf([P, M], I32, "w8_codes")
+        w4_codes = sbuf([P, 2, M // 2], I32, "w4_codes")
+        quarters = [(g, h) for h in range(2) for g in range(2)]
+        prev_sb = [sbuf([P, 4, HALF], F32, f"prev_sb{h}") for h in range(2)]
+
+        nc.vector.memset(table_scales[0:32], 0)
+        nc.vector.memset(w4_planes[0:64], 0)
+        nc.vector.memset(w8_plane[:], 0)
 
         raws = {}
 
         def load_w1(b, a, c0, c1):
-            raw = keep.tile([P, 4, c1 - c0], F32, name=f"raw{b}{a}_{c0}", align_bytes=ALIGN)
+            if (b, a, c1) == (LAST, 1, PASS):
+                raw = last.tile([P, 4, c1 - c0], F32, name="last_raw", align_bytes=ALIGN, offset=0)
+            else:
+                raw = sbuf([P, 4, c1 - c0], F32, f"raw{b}{a}_{c0}")
             rows = w1[PASS * a : PASS * (a + 1), PASS * b + c0 : PASS * b + c1]
             nc.sync.dma_start(raw[:], rows.rearrange("(p j) c -> p j c", j=4))
             raws[b, a, c0] = raw
 
-        def load_scale_rows(tile, planes, rows):
-            by_r = rows.rearrange("a (q r) c -> r q a c", r=4)
-            for r in range(4):
-                nc.sync.dma_start(tile[r:P:32, planes, :], by_r[r])
+        def quarter(dram, g, h):
+            return dram[256 * g : 256 * (g + 1), HALF * h : HALF * (h + 1)].rearrange("(m p) j -> p m j", p=P)
 
         tab_i32 = tab.bitcast(I32)
-        tab_scale_rows = tab_i32[:, WORD_BYTES // 4 :].rearrange("a (q c) -> a q c", q=16)
-        w8_rows = w8_scales.bitcast(I32)
-        w4_rows = w4_scales.bitcast(I32)
-
         nc.sync.dma_start(table_words[:], tab_i32[:, 0 : WORD_BYTES // 4].rearrange("a (p c) -> p a c", p=P))
         nc.sync.dma_start(offsets[:], offs)
-        load_w1(FIRST, 0, 0, PASS)
-        load_scale_rows(table_scales, slice(0, 2), tab_scale_rows)
-        load_w1(FIRST, 1, 0, PASS)
-        load_w1(SECOND, 0, 0, PASS)
-        load_w1(SECOND, 1, 0, PASS)
+        for a in range(2):
+            rows = tab_i32[a, WORD_BYTES // 4 :].rearrange("(q r c) -> r q c", q=4, r=4)
+            nc.sync.dma_start(table_scales[4 * a : 4 * a + 4], rows)
+        for b in (FIRST, SECOND):
+            for a in range(2):
+                load_w1(b, a, 0, PASS)
         load_w1(LAST, 0, 0, 256)
         load_w1(LAST, 0, 256, 512)
         load_w1(LAST, 1, 0, 256)
         load_w1(LAST, 1, 256, 384)
         load_w1(LAST, 1, 384, 512)
-        load_scale_rows(w2_scales, slice(1, 3), w4_rows)
+        w4_rows = w4_scales.bitcast(I32).rearrange("a (u q r) c -> q r (a u) c", u=2, q=2)
+        for q in range(2):
+            nc.sync.dma_start(w4_planes[32 * q : 32 * q + 4].rearrange("r a u c -> r (a u) c"), w4_rows[q])
         nc.sync.dma_start(w4_codes[:], w4_words.bitcast(I32).rearrange("a p c -> p a c"))
+        nc.sync.dma_start(w8_rows[:], w8_scales.bitcast(I32)[0].rearrange("(q r) c -> r q c", r=4))
         nc.sync.dma_start(w8_codes[:], w8_words[0].rearrange("p n i -> p (n i)").bitcast(I32))
-        nc.sync.dma_start(prev_sb[0][:], prev[0:256, :].rearrange("(m p) j -> p m j", p=P))
-        load_scale_rows(w2_scales, slice(0, 1), w8_rows)
-        nc.sync.dma_start(prev_sb[1][:], prev[256:512, :].rearrange("(m p) j -> p m j", p=P))
+        for h in range(2):
+            nc.sync.dma_start(prev_sb[h][:], prev[:, HALF * h : HALF * (h + 1)].rearrange("(m p) j -> p m j", p=P))
 
+        for q in range(1, 4):
+            nc.vector.tensor_copy(table_scales[32 * q : 32 * (q + 1), 0, :], table_scales[0:32, q, :])
         picked_words = []
         for a in range(2):
-            words = keep.tile([P, S], U32, name=f"picked_words{a}", align_bytes=ALIGN)
+            words = sbuf([P, S], U32, f"picked_words{a}")
             nc.vector.tensor_copy(words[:], table_words[:, a, :].bitcast(U32).indirect(offsets[:]))
             picked_words.append(words)
-        picked_scales = []
-        for a in range(2):
-            scale_bytes = keep.tile([P, S], U8, name=f"picked_scales{a}", align_bytes=ALIGN)
-            nc.vector.tensor_copy(scale_bytes[:], table_scales[:, a, :].bitcast(U8).indirect(offsets[:]))
-            picked_scales.append(scale_bytes)
+        picked_scales = sbuf([P, S], U8, "picked_scales")
+        nc.vector.tensor_copy(picked_scales[:], table_scales[:, 0, :].bitcast(U8).indirect(offsets[:]))
 
         grouped, codes, scales = {}, {}, {}
         for b in range(3):
             for a in range(2):
                 for u in range(2):
-                    grouped[b, a, u] = keep.tile([P, 1024], BF16, name=f"grouped{b}{a}{u}", align_bytes=ALIGN)
-                codes[b, a] = keep.tile([P, PASS], U32, name=f"w1_codes{b}{a}", align_bytes=ALIGN)
-                scales[b, a] = keep.tile([P, PASS], U8, name=f"w1_scales{b}{a}", align_bytes=ALIGN)
+                    grouped[b, a, u] = sbuf([P, 1024], BF16, f"grouped{b}{a}{u}")
+                codes[b, a] = sbuf([P, PASS], U32, f"w1_codes{b}{a}")
+                scales[b, a] = sbuf([P, PASS], U8, f"w1_scales{b}{a}")
 
         def interleave(engine, b, a, c0, u, m0, m1):
             dst = grouped[b, a, u][:].rearrange("p (t m j) -> p m j t", t=2, j=4)[:, m0:m1]
@@ -146,7 +153,7 @@ def tile_list_tabmlp_mix_res_kernel(
                     lhsT=codes[b, a][:, cols].bitcast(FP8),
                     lhsT_scale=scales[b, a][:, cols],
                     rhs=picked_words[a][:, toks].bitcast(FP8),
-                    rhs_scale=picked_scales[a][:, toks],
+                    rhs_scale=picked_scales[4 * a : P, toks],
                     start=(a, t, h) == of_bank[0],
                     stop=(a, t, h) == of_bank[-1],
                 )
@@ -157,23 +164,14 @@ def tile_list_tabmlp_mix_res_kernel(
 
         h_grouped, h_codes, h_scales = {}, {}, {}
         for b in range(3):
-            h_scales[b] = keep.tile([P, S], U8, name=f"h_scales{b}", align_bytes=ALIGN)
+            h_scales[b] = sbuf([P, S], U8, f"h_scales{b}")
 
-        def relu(engine, b, h, dst):
+        def relu(b, h, dst):
             h_grouped[b, h] = dst
-            src = banks[b, h][:].rearrange("p t n -> p n t")
-            if engine is nc.scalar:
-                nc.scalar.activation(dst, src, RELU)
-            else:
-                nc.vector.tensor_scalar_max(dst, src, 0.0)
+            nc.scalar.activation(dst, banks[b, h][:].rearrange("p t n -> p n t"), RELU)
 
-        def relu_tile(tag):
-            tile = keep.tile([P, HALF, 4], BF16, name=tag, align_bytes=ALIGN)
-            return tile[:]
-
-        def codes_tile(tag, width):
-            tile = keep.tile([P, width], U32, name=tag, align_bytes=ALIGN)
-            return tile[:]
+        def codes_tile(tag):
+            return sbuf([P, HALF], U32, tag)[:]
 
         def hidden_quantise(b, h, dst):
             h_codes[b, h] = dst
@@ -183,28 +181,25 @@ def tile_list_tabmlp_mix_res_kernel(
                 in_=h_grouped[b, h].rearrange("p n t -> p (n t)"),
             )
 
-        halves = [slice(0, HALF), slice(HALF, S)]
-        both_halves = slice(0, S)
-
         for a in range(2):
             share_copies(FIRST, a, 0, PASS, EXTRA_WHOLE)
             quantise_part(FIRST, a)
         hidden_matmuls(FIRST, early_first_bank)
         share_copies(SECOND, 0, 0, PASS, EXTRA_WHOLE)
         quantise_part(SECOND, 0)
-        first_h = keep.tile([P, 2, HALF, 4], BF16, name=f"raw{SECOND}0_0", align_bytes=ALIGN)
+        first_h = sbuf([P, 2, HALF, 4], BF16, f"raw{SECOND}0_0")
         for h in range(2):
-            relu(nc.scalar, FIRST, h, first_h[:, h])
-        hidden_quantise(FIRST, 0, codes_tile(f"grouped{SECOND}01", HALF))
+            relu(FIRST, h, first_h[:, h])
+        hidden_quantise(FIRST, 0, codes_tile(f"grouped{SECOND}01"))
         share_copies(SECOND, 1, 0, PASS, EXTRA_FOURTH)
         quantise_part(SECOND, 1)
-        hidden_quantise(FIRST, 1, codes_tile(f"raw{SECOND}1_0", HALF))
+        hidden_quantise(FIRST, 1, codes_tile(f"raw{SECOND}1_0"))
         hidden_matmuls(SECOND, one_stretch)
 
         share_copies(LAST, 0, 0, 256, 0)
         share_copies(LAST, 0, 256, 512, EXTRA_HALF)
         quantise_part(LAST, 0)
-        relu(nc.scalar, SECOND, 0, relu_tile(f"raw{LAST}0_256"))
+        relu(SECOND, 0, sbuf([P, HALF, 4], BF16, f"raw{LAST}0_256")[:])
         share_copies(LAST, 1, 0, 256, EXTRA_HALF)
         share_copies(LAST, 1, 256, 384, 0)
         quantise_half_slices(0, 0)
@@ -212,66 +207,60 @@ def tile_list_tabmlp_mix_res_kernel(
         quantise_half_slices(1, 0)
         quantise_half_slices(0, 1)
         quantise_half_slices(1, 1)
-        relu(nc.scalar, SECOND, 1, relu_tile(f"raw{LAST}1_384"))
+        relu(SECOND, 1, last.tile([P, HALF, 4], BF16, name="second_h1", align_bytes=ALIGN, offset=0)[:])
         hidden_matmuls(LAST, early_first_bank)
-        second_h = codes_tile(f"grouped{LAST}11", S)
-        hidden_quantise(SECOND, 0, second_h[:, halves[0]])
-        relu(nc.vector, LAST, 0, relu_tile("h_grouped0"))
-        hidden_quantise(SECOND, 1, second_h[:, halves[1]])
-        relu(nc.scalar, LAST, 1, relu_tile("h_grouped1"))
-
-        whole = {m: psum.tile([P, S], F32, name=f"out{m}") for m in range(1, 4)}
-        sums = {(m, h): whole[m][:, halves[h]] for m in range(1, 4) for h in range(2)}
-        sums[0, 0] = psum.tile([P, HALF], F32, name="out0")[:]
-        sums[0, 1] = psum.tile([P, HALF], F32, name="hidden10")[:]
-
-        def out_matmul(dst, m, b, moving, toks, start, stop):
-            if b == 0:
-                weights = w8_codes[:, HALF * m : HALF * (m + 1)].bitcast(FP8)
-            else:
-                weights = w4_codes[:, b - 1, 64 * m : 64 * (m + 1)].bitcast(FP4)
-            nc.tensor.matmul_mx(
-                out=dst,
-                lhsT=weights,
-                lhsT_scale=w2_scales[:, b, 32 * m : 32 * (m + 1)].bitcast(U8),
-                rhs=moving.bitcast(FP8),
-                rhs_scale=h_scales[b][:, toks],
-                start=start,
-                stop=stop,
-            )
-
-        def half_pass(m, h, b, start=False, stop=False):
-            out_matmul(sums[m, h], m, b, h_codes[b, h], halves[h], start, stop)
-
-        def closing_pass(m):
-            out_matmul(whole[m][:], m, LAST, last_h, both_halves, False, True)
-
-        def finish(total, m, toks, queue):
-            width = toks.stop - toks.start
-            result = keep.tile([P, width], F32, name=f"result{m}_{toks.start}", align_bytes=ALIGN)
-            nc.vector.tensor_add(result[:], total, prev_sb[m // 2][:, m % 2, toks])
-            queue.dma_start(out[P * m : P * (m + 1), toks], result[:])
-
-        for m in range(4):
-            half_pass(m, 0, SECOND, start=True)
-            half_pass(m, 0, FIRST)
-            if m > 0:
-                half_pass(m, 1, FIRST)
-        for m in (1, 2):
-            half_pass(m, 1, SECOND)
-        last_h = codes_tile("h_codes_last", S)
+        hidden_quantise(SECOND, 0, last.tile([P, HALF], U32, name="second_codes0", align_bytes=ALIGN, offset=1024)[:])
+        for a in range(2):
+            nc.vector.tensor_copy(w4_planes[64:P, a, 0, :], w4_planes[0:64, a, 1, :])
+        for q in range(4):
+            nc.vector.tensor_copy(w8_plane[32 * q : 32 * q + 4, :], w8_rows[:, q, :])
         for h in range(2):
-            hidden_quantise(LAST, h, last_h[:, halves[h]])
-        half_pass(0, 0, LAST, stop=True)
-        for m in (1, 2):
-            closing_pass(m)
-        half_pass(3, 1, SECOND)
-        closing_pass(3)
-        half_pass(0, 1, SECOND, start=True)
-        half_pass(0, 1, FIRST)
-        half_pass(0, 1, LAST, stop=True)
+            relu(LAST, h, sbuf([P, HALF, 4], BF16, f"h_grouped{h}")[:])
+        for i, (b, h) in enumerate(((LAST, 0), (SECOND, 1), (LAST, 1))):
+            tile = rows_pool.tile([P, HALF], U32, name=f"late_codes{i}", align_bytes=ALIGN, offset=4 * HALF * i)
+            hidden_quantise(b, h, tile[:])
 
-        finish(sums[0, 0], 0, halves[0], nc.sync)
-        for m, queue in ((1, nc.scalar), (2, nc.sync), (3, nc.scalar)):
-            finish(whole[m][:], m, both_halves, queue)
-        finish(sums[0, 1], 0, halves[1], nc.sync)
+        bank_tags = {(0, 0): "out0", (1, 0): "out1", (0, 1): "out2", (1, 1): "out3"}
+        sums = {q: psum.tile([P, 2, HALF], F32, name=bank_tags[q]) for q in quarters}
+        block_order = {
+            (0, 0): (FIRST, SECOND, LAST),
+            (1, 0): (FIRST, SECOND, LAST),
+            (0, 1): (FIRST, SECOND, LAST),
+            (1, 1): (SECOND, FIRST, LAST),
+        }
+
+        def out_passes(g, h, step):
+            b = block_order[g, h][step]
+            for i in range(2):
+                m = 2 * g + i
+                if b == LAST:
+                    weights = w8_codes[:, HALF * m : HALF * (m + 1)].bitcast(FP8)
+                    plane = w8_plane[:]
+                else:
+                    weights = w4_codes[:, b - 1, 64 * m : 64 * (m + 1)].bitcast(FP4)
+                    plane = w4_planes[:, b - 1, 0, :]
+                nc.tensor.matmul_mx(
+                    out=sums[g, h][:, i, :],
+                    lhsT=weights,
+                    lhsT_scale=plane[:, 32 * m : 32 * (m + 1)].bitcast(U8),
+                    rhs=h_codes[b, h].bitcast(FP8),
+                    rhs_scale=h_scales[b][:, HALF * h : HALF * (h + 1)],
+                    start=(step, i) == (0, 0),
+                    stop=(step, i) == (2, 1),
+                )
+
+        for step in range(2):
+            for g in range(2):
+                out_passes(g, 0, step)
+        out_passes(0, 1, 0)
+        for g in range(2):
+            out_passes(g, 0, 2)
+        out_passes(0, 1, 1)
+        out_passes(0, 1, 2)
+        for step in range(3):
+            out_passes(1, 1, step)
+
+        for g, h in quarters:
+            result = sbuf([P, 2, HALF], F32, f"result{g}{h}")
+            nc.vector.tensor_add(result[:], sums[g, h][:], prev_sb[h][:, 2 * g : 2 * g + 2])
+            nc.sync.dma_start(quarter(out, g, h), result[:])

@@ -40,18 +40,17 @@ def tile_list_tabmlp_mix_res_kernel(
 
         offsets = keep.tile([P, S // 16], U16, name="offsets")
         table_words = sbuf([P, 2, T], I32, "table_words")
-        table_scales = sbuf([P, 4, T // 4], I32, "table_scales")
-        w4_planes = sbuf([P, 2, 2, M // 4], I32, "w4_planes")
-        w8_plane = sbuf([P, M // 4], I32, "w8_plane")
+        table_scales = sbuf([P, 2, T // 4], I32, "table_scales")
+        w2_planes = sbuf([P, 3, M // 4], I32, "w2_planes")
         w8_rows = rows_pool.tile([4, 4, M // 4], I32, name="w8_rows", align_bytes=ALIGN, offset=0)
         w8_codes = sbuf([P, M], I32, "w8_codes")
         w4_codes = sbuf([P, 2, M // 2], I32, "w4_codes")
         quarters = [(g, h) for h in range(2) for g in range(2)]
-        prev_sb = [sbuf([P, 4, HALF], F32, f"prev_sb{h}") for h in range(2)]
+        pieces = [(0, 0, 0, 1), (0, 0, 1, 2)] + [(g, h, 0, 2) for g, h in quarters[1:]]
+        prev_sb = {(g, h, i0): sbuf([P, i1 - i0, HALF], F32, f"prev_sb{g}{h}{i0}") for g, h, i0, i1 in pieces}
 
-        nc.vector.memset(table_scales[0:32], 0)
-        nc.vector.memset(w4_planes[0:64], 0)
-        nc.vector.memset(w8_plane[:], 0)
+        nc.vector.memset(table_scales[:], 0)
+        nc.vector.memset(w2_planes[:], 0)
 
         raws = {}
 
@@ -64,41 +63,44 @@ def tile_list_tabmlp_mix_res_kernel(
             nc.sync.dma_start(raw[:], rows.rearrange("(p j) c -> p j c", j=4))
             raws[b, a, c0] = raw
 
+        def load_scale_rows(planes, rows):
+            by_r = rows.rearrange("a (q r) c -> r q a c", r=4)
+            for r in range(4):
+                nc.sync.dma_start(planes[r:P:32], by_r[r])
+
         def quarter(dram, g, h):
             return dram[256 * g : 256 * (g + 1), HALF * h : HALF * (h + 1)].rearrange("(m p) j -> p m j", p=P)
 
         tab_i32 = tab.bitcast(I32)
         nc.sync.dma_start(table_words[:], tab_i32[:, 0 : WORD_BYTES // 4].rearrange("a (p c) -> p a c", p=P))
         nc.sync.dma_start(offsets[:], offs)
+        load_w1(FIRST, 0, 0, PASS)
+        load_scale_rows(table_scales[:], tab_i32[:, WORD_BYTES // 4 :].rearrange("a (q c) -> a q c", q=16))
+        load_w1(FIRST, 1, 0, PASS)
         for a in range(2):
-            rows = tab_i32[a, WORD_BYTES // 4 :].rearrange("(q r c) -> r q c", q=4, r=4)
-            nc.sync.dma_start(table_scales[4 * a : 4 * a + 4], rows)
-        for b in (FIRST, SECOND):
-            for a in range(2):
-                load_w1(b, a, 0, PASS)
+            load_w1(SECOND, a, 0, PASS)
         load_w1(LAST, 0, 0, 256)
         load_w1(LAST, 0, 256, 512)
         load_w1(LAST, 1, 0, 256)
         load_w1(LAST, 1, 256, 384)
         load_w1(LAST, 1, 384, 512)
-        w4_rows = w4_scales.bitcast(I32).rearrange("a (u q r) c -> q r (a u) c", u=2, q=2)
-        for q in range(2):
-            nc.sync.dma_start(w4_planes[32 * q : 32 * q + 4].rearrange("r a u c -> r (a u) c"), w4_rows[q])
-        nc.sync.dma_start(w4_codes[:], w4_words.bitcast(I32).rearrange("a p c -> p a c"))
+        load_scale_rows(w2_planes[:, 1:3], w4_scales.bitcast(I32))
         nc.sync.dma_start(w8_rows[:], w8_scales.bitcast(I32)[0].rearrange("(q r) c -> r q c", r=4))
+        nc.sync.dma_start(w4_codes[:], w4_words.bitcast(I32).rearrange("a p c -> p a c"))
         nc.sync.dma_start(w8_codes[:], w8_words[0].rearrange("p n i -> p (n i)").bitcast(I32))
-        for h in range(2):
-            nc.sync.dma_start(prev_sb[h][:], prev[:, HALF * h : HALF * (h + 1)].rearrange("(m p) j -> p m j", p=P))
+        for g, h, i0, i1 in pieces:
+            nc.sync.dma_start(prev_sb[g, h, i0][:], quarter(prev, g, h)[:, i0:i1])
 
-        for q in range(1, 4):
-            nc.vector.tensor_copy(table_scales[32 * q : 32 * (q + 1), 0, :], table_scales[0:32, q, :])
         picked_words = []
         for a in range(2):
             words = sbuf([P, S], U32, f"picked_words{a}")
             nc.vector.tensor_copy(words[:], table_words[:, a, :].bitcast(U32).indirect(offsets[:]))
             picked_words.append(words)
-        picked_scales = sbuf([P, S], U8, "picked_scales")
-        nc.vector.tensor_copy(picked_scales[:], table_scales[:, 0, :].bitcast(U8).indirect(offsets[:]))
+        picked_scales = []
+        for a in range(2):
+            scale_bytes = sbuf([P, S], U8, f"picked_scales{a}")
+            nc.vector.tensor_copy(scale_bytes[:], table_scales[:, a, :].bitcast(U8).indirect(offsets[:]))
+            picked_scales.append(scale_bytes)
 
         grouped, codes, scales = {}, {}, {}
         for b in range(3):
@@ -153,7 +155,7 @@ def tile_list_tabmlp_mix_res_kernel(
                     lhsT=codes[b, a][:, cols].bitcast(FP8),
                     lhsT_scale=scales[b, a][:, cols],
                     rhs=picked_words[a][:, toks].bitcast(FP8),
-                    rhs_scale=picked_scales[4 * a : P, toks],
+                    rhs_scale=picked_scales[a][:, toks],
                     start=(a, t, h) == of_bank[0],
                     stop=(a, t, h) == of_bank[-1],
                 )
@@ -210,10 +212,8 @@ def tile_list_tabmlp_mix_res_kernel(
         relu(SECOND, 1, last.tile([P, HALF, 4], BF16, name="second_h1", align_bytes=ALIGN, offset=0)[:])
         hidden_matmuls(LAST, early_first_bank)
         hidden_quantise(SECOND, 0, last.tile([P, HALF], U32, name="second_codes0", align_bytes=ALIGN, offset=1024)[:])
-        for a in range(2):
-            nc.vector.tensor_copy(w4_planes[64:P, a, 0, :], w4_planes[0:64, a, 1, :])
         for q in range(4):
-            nc.vector.tensor_copy(w8_plane[32 * q : 32 * q + 4, :], w8_rows[:, q, :])
+            nc.vector.tensor_copy(w2_planes[32 * q : 32 * q + 4, LAST, :], w8_rows[:, q, :])
         for h in range(2):
             relu(LAST, h, sbuf([P, HALF, 4], BF16, f"h_grouped{h}")[:])
         for i, (b, h) in enumerate(((LAST, 0), (SECOND, 1), (LAST, 1))):
@@ -235,14 +235,12 @@ def tile_list_tabmlp_mix_res_kernel(
                 m = 2 * g + i
                 if b == LAST:
                     weights = w8_codes[:, HALF * m : HALF * (m + 1)].bitcast(FP8)
-                    plane = w8_plane[:]
                 else:
                     weights = w4_codes[:, b - 1, 64 * m : 64 * (m + 1)].bitcast(FP4)
-                    plane = w4_planes[:, b - 1, 0, :]
                 nc.tensor.matmul_mx(
                     out=sums[g, h][:, i, :],
                     lhsT=weights,
-                    lhsT_scale=plane[:, 32 * m : 32 * (m + 1)].bitcast(U8),
+                    lhsT_scale=w2_planes[:, b, 32 * m : 32 * (m + 1)].bitcast(U8),
                     rhs=h_codes[b, h].bitcast(FP8),
                     rhs_scale=h_scales[b][:, HALF * h : HALF * (h + 1)],
                     start=(step, i) == (0, 0),
@@ -260,7 +258,7 @@ def tile_list_tabmlp_mix_res_kernel(
         for step in range(3):
             out_passes(1, 1, step)
 
-        for g, h in quarters:
-            result = sbuf([P, 2, HALF], F32, f"result{g}{h}")
-            nc.vector.tensor_add(result[:], sums[g, h][:], prev_sb[h][:, 2 * g : 2 * g + 2])
-            nc.sync.dma_start(quarter(out, g, h), result[:])
+        for g, h, i0, i1 in pieces:
+            result = sbuf([P, i1 - i0, HALF], F32, f"result{g}{h}{i0}")
+            nc.vector.tensor_add(result[:], sums[g, h][:, i0:i1], prev_sb[g, h, i0][:])
+            nc.sync.dma_start(quarter(out, g, h)[:, i0:i1], result[:])

@@ -42,12 +42,11 @@ def tile_list_tabmlp_mix_res_kernel(
         table_words = sbuf([P, 2, T], I32, "table_words")
         table_scales = sbuf([P, 2, T // 4], I32, "table_scales")
         w2_planes = sbuf([P, 3, M // 4], I32, "w2_planes")
-        w8_rows = rows_pool.tile([4, 4, M // 4], I32, name="w8_rows", align_bytes=ALIGN, offset=0)
         w8_codes = sbuf([P, M], I32, "w8_codes")
         w4_codes = sbuf([P, 2, M // 2], I32, "w4_codes")
         quarters = [(g, h) for h in range(2) for g in range(2)]
         pieces = [(0, 0, 0, 1), (0, 0, 1, 2)] + [(g, h, 0, 2) for g, h in quarters[1:]]
-        prev_sb = {(g, h, i0): sbuf([P, i1 - i0, HALF], F32, f"prev_sb{g}{h}{i0}") for g, h, i0, i1 in pieces}
+        prev_sb = [sbuf([P, 4, HALF], F32, f"prev_sb{h}") for h in range(2)]
 
         nc.vector.memset(table_scales[:], 0)
         nc.vector.memset(w2_planes[:], 0)
@@ -79,17 +78,17 @@ def tile_list_tabmlp_mix_res_kernel(
         load_w1(FIRST, 1, 0, PASS)
         for a in range(2):
             load_w1(SECOND, a, 0, PASS)
+        load_scale_rows(w2_planes[:, 0:1], w8_scales.bitcast(I32))
         load_w1(LAST, 0, 0, 256)
         load_w1(LAST, 0, 256, 512)
         load_w1(LAST, 1, 0, 256)
         load_w1(LAST, 1, 256, 384)
         load_w1(LAST, 1, 384, 512)
         load_scale_rows(w2_planes[:, 1:3], w4_scales.bitcast(I32))
-        nc.sync.dma_start(w8_rows[:], w8_scales.bitcast(I32)[0].rearrange("(q r) c -> r q c", r=4))
         nc.sync.dma_start(w4_codes[:], w4_words.bitcast(I32).rearrange("a p c -> p a c"))
         nc.sync.dma_start(w8_codes[:], w8_words[0].rearrange("p n i -> p (n i)").bitcast(I32))
-        for g, h, i0, i1 in pieces:
-            nc.sync.dma_start(prev_sb[g, h, i0][:], quarter(prev, g, h)[:, i0:i1])
+        for h in range(2):
+            nc.sync.dma_start(prev_sb[h][:], prev[:, HALF * h : HALF * (h + 1)].rearrange("(m p) j -> p m j", p=P))
 
         picked_words = []
         for a in range(2):
@@ -106,7 +105,10 @@ def tile_list_tabmlp_mix_res_kernel(
         for b in range(3):
             for a in range(2):
                 for u in range(2):
-                    grouped[b, a, u] = sbuf([P, 1024], BF16, f"grouped{b}{a}{u}")
+                    if (b, a, u) == (SECOND, 0, 1):
+                        grouped[b, a, u] = rows_pool.tile([P, 1024], BF16, name="third", align_bytes=ALIGN, offset=0)
+                    else:
+                        grouped[b, a, u] = sbuf([P, 1024], BF16, f"grouped{b}{a}{u}")
                 codes[b, a] = sbuf([P, PASS], U32, f"w1_codes{b}{a}")
                 scales[b, a] = sbuf([P, PASS], U8, f"w1_scales{b}{a}")
 
@@ -192,7 +194,7 @@ def tile_list_tabmlp_mix_res_kernel(
         first_h = sbuf([P, 2, HALF, 4], BF16, f"raw{SECOND}0_0")
         for h in range(2):
             relu(FIRST, h, first_h[:, h])
-        hidden_quantise(FIRST, 0, codes_tile(f"grouped{SECOND}01"))
+        hidden_quantise(FIRST, 0, rows_pool.tile([P, HALF], U32, name="first_codes0", align_bytes=ALIGN, offset=256)[:])
         share_copies(SECOND, 1, 0, PASS, EXTRA_FOURTH)
         quantise_part(SECOND, 1)
         hidden_quantise(FIRST, 1, codes_tile(f"raw{SECOND}1_0"))
@@ -212,13 +214,9 @@ def tile_list_tabmlp_mix_res_kernel(
         relu(SECOND, 1, last.tile([P, HALF, 4], BF16, name="second_h1", align_bytes=ALIGN, offset=0)[:])
         hidden_matmuls(LAST, early_first_bank)
         hidden_quantise(SECOND, 0, last.tile([P, HALF], U32, name="second_codes0", align_bytes=ALIGN, offset=1024)[:])
-        for q in range(4):
-            nc.vector.tensor_copy(w2_planes[32 * q : 32 * q + 4, LAST, :], w8_rows[:, q, :])
         for h in range(2):
             relu(LAST, h, sbuf([P, HALF, 4], BF16, f"h_grouped{h}")[:])
-        for i, (b, h) in enumerate(((LAST, 0), (SECOND, 1), (LAST, 1))):
-            tile = rows_pool.tile([P, HALF], U32, name=f"late_codes{i}", align_bytes=ALIGN, offset=4 * HALF * i)
-            hidden_quantise(b, h, tile[:])
+        hidden_quantise(LAST, 0, codes_tile("last_codes0"))
 
         bank_tags = {(0, 0): "out0", (1, 0): "out1", (0, 1): "out2", (1, 1): "out3"}
         sums = {q: psum.tile([P, 2, HALF], F32, name=bank_tags[q]) for q in quarters}
@@ -250,6 +248,9 @@ def tile_list_tabmlp_mix_res_kernel(
         for step in range(2):
             for g in range(2):
                 out_passes(g, 0, step)
+        for i, b in enumerate((SECOND, LAST)):
+            tile = rows_pool.tile([P, HALF], U32, name=f"late_codes{i}", align_bytes=ALIGN, offset=4 * HALF * i)
+            hidden_quantise(b, 1, tile[:])
         out_passes(0, 1, 0)
         for g in range(2):
             out_passes(g, 0, 2)
@@ -260,5 +261,5 @@ def tile_list_tabmlp_mix_res_kernel(
 
         for g, h, i0, i1 in pieces:
             result = sbuf([P, i1 - i0, HALF], F32, f"result{g}{h}{i0}")
-            nc.vector.tensor_add(result[:], sums[g, h][:, i0:i1], prev_sb[g, h, i0][:])
+            nc.vector.tensor_add(result[:], sums[g, h][:, i0:i1], prev_sb[h][:, 2 * g + i0 : 2 * g + i1])
             nc.sync.dma_start(quarter(out, g, h)[:, i0:i1], result[:])

@@ -138,6 +138,11 @@ def tile_list_tabmlp_mix_res_kernel(
             for u in range(2):
                 quantise(b, a, u, 0, 1024)
 
+        def quantise_slices(b, a):
+            for u in range(2):
+                for t in range(2):
+                    quantise(b, a, u, 512 * t, 512 * (t + 1))
+
         def quantise_half_slices(u, upper):
             for t in range(2):
                 quantise(LAST, 1, u, 512 * t + 256 * upper, 512 * t + 256 * (upper + 1))
@@ -187,10 +192,10 @@ def tile_list_tabmlp_mix_res_kernel(
 
         for a in range(2):
             share_copies(FIRST, a, 0, PASS, EXTRA_WHOLE)
-            quantise_part(FIRST, a)
+            quantise_slices(FIRST, a)
         hidden_matmuls(FIRST, early_first_bank)
         share_copies(SECOND, 0, 0, PASS, EXTRA_WHOLE)
-        quantise_part(SECOND, 0)
+        quantise_slices(SECOND, 0)
         first_h = sbuf([P, 2, HALF, 4], BF16, f"raw{SECOND}0_0")
         for h in range(2):
             relu(FIRST, h, first_h[:, h])

@@ -41,7 +41,9 @@ def tile_list_tabmlp_mix_res_kernel(
         offsets = keep.tile([P, S // 16], U16, name="offsets")
         table_words = sbuf([P, 2, T], I32, "table_words")
         table_scales = sbuf([P, 2, T // 4], I32, "table_scales")
-        w2_planes = sbuf([P, 3, M // 4], I32, "w2_planes")
+        w2_planes = sbuf([P, 2 * (M // 4) + HALF // 4], I32, "w2_planes")
+        w4_planes = w2_planes[:, 0 : 2 * (M // 4)].rearrange("p (a c) -> p a c", a=2)
+        w8_planes = w2_planes[:, 2 * (M // 4) :]
         w8_codes = sbuf([P, M], I32, "w8_codes")
         w4_codes = sbuf([P, 2, M // 2], I32, "w4_codes")
         quarters = [(g, h) for h in range(2) for g in range(2)]
@@ -78,13 +80,15 @@ def tile_list_tabmlp_mix_res_kernel(
         load_w1(FIRST, 1, 0, PASS)
         for a in range(2):
             load_w1(SECOND, a, 0, PASS)
-        load_scale_rows(w2_planes[:, 0:1], w8_scales.bitcast(I32))
+        w8_rows = w8_scales.bitcast(I32)[0].rearrange("(q r) (m c) -> q m r c", r=4, m=4)
+        for q in range(4):
+            nc.sync.dma_start(w8_planes[32 * q : 32 * q + 16], w8_rows[q])
         load_w1(LAST, 0, 0, 256)
         load_w1(LAST, 0, 256, 512)
         load_w1(LAST, 1, 0, 256)
         load_w1(LAST, 1, 256, 384)
         load_w1(LAST, 1, 384, 512)
-        load_scale_rows(w2_planes[:, 1:3], w4_scales.bitcast(I32))
+        load_scale_rows(w4_planes, w4_scales.bitcast(I32))
         nc.sync.dma_start(w4_codes[:], w4_words.bitcast(I32).rearrange("a p c -> p a c"))
         nc.sync.dma_start(w8_codes[:], w8_words[0].rearrange("p n i -> p (n i)").bitcast(I32))
         for h in range(2):
@@ -195,7 +199,7 @@ def tile_list_tabmlp_mix_res_kernel(
             quantise_slices(FIRST, a)
         hidden_matmuls(FIRST, early_first_bank)
         share_copies(SECOND, 0, 0, PASS, EXTRA_WHOLE)
-        quantise_slices(SECOND, 0)
+        quantise_part(SECOND, 0)
         first_h = sbuf([P, 2, HALF, 4], BF16, f"raw{SECOND}0_0")
         for h in range(2):
             relu(FIRST, h, first_h[:, h])
@@ -221,7 +225,7 @@ def tile_list_tabmlp_mix_res_kernel(
         hidden_quantise(SECOND, 0, last.tile([P, HALF], U32, name="second_codes0", align_bytes=ALIGN, offset=1024)[:])
         for h in range(2):
             relu(LAST, h, sbuf([P, HALF, 4], BF16, f"h_grouped{h}")[:])
-        hidden_quantise(LAST, 0, codes_tile("last_codes0"))
+        hidden_quantise(LAST, 0, codes_tile(f"w1_codes{LAST}1"))
 
         bank_tags = {(0, 0): "out0", (1, 0): "out1", (0, 1): "out2", (1, 1): "out3"}
         sums = {q: psum.tile([P, 2, HALF], F32, name=bank_tags[q]) for q in quarters}
@@ -238,12 +242,14 @@ def tile_list_tabmlp_mix_res_kernel(
                 m = 2 * g + i
                 if b == LAST:
                     weights = w8_codes[:, HALF * m : HALF * (m + 1)].bitcast(FP8)
+                    plane = w8_planes[4 * m : P]
                 else:
                     weights = w4_codes[:, b - 1, 64 * m : 64 * (m + 1)].bitcast(FP4)
+                    plane = w4_planes[:, b - 1, 32 * m : 32 * (m + 1)]
                 nc.tensor.matmul_mx(
                     out=sums[g, h][:, i, :],
                     lhsT=weights,
-                    lhsT_scale=w2_planes[:, b, 32 * m : 32 * (m + 1)].bitcast(U8),
+                    lhsT_scale=plane.bitcast(U8),
                     rhs=h_codes[b, h].bitcast(FP8),
                     rhs_scale=h_scales[b][:, HALF * h : HALF * (h + 1)],
                     start=(step, i) == (0, 0),

@@ -51,7 +51,8 @@ def tile_list_tabmlp_mix_res_kernel(
         prev_sb = [sbuf([P, 4, HALF], F32, f"prev_sb{h}") for h in range(2)]
 
         nc.vector.memset(table_scales[:], 0)
-        nc.vector.memset(w2_planes[:], 0)
+        nc.vector.memset(w8_planes, 0)
+        nc.vector.memset(w4_planes, 0)
 
         raws = {}
 
@@ -110,7 +111,7 @@ def tile_list_tabmlp_mix_res_kernel(
             for a in range(2):
                 for u in range(2):
                     if (b, a, u) == (SECOND, 0, 1):
-                        grouped[b, a, u] = rows_pool.tile([P, 1024], BF16, name="third", align_bytes=ALIGN, offset=0)
+                        grouped[b, a, u] = rows_pool.tile([P, 1024], BF16, name="third", align_bytes=ALIGN, offset=2048)
                     else:
                         grouped[b, a, u] = sbuf([P, 1024], BF16, f"grouped{b}{a}{u}")
                 codes[b, a] = sbuf([P, PASS], U32, f"w1_codes{b}{a}")
@@ -196,14 +197,14 @@ def tile_list_tabmlp_mix_res_kernel(
 
         for a in range(2):
             share_copies(FIRST, a, 0, PASS, EXTRA_WHOLE)
-            quantise_slices(FIRST, a)
+            (quantise_part if a else quantise_slices)(FIRST, a)
         hidden_matmuls(FIRST, early_first_bank)
         share_copies(SECOND, 0, 0, PASS, EXTRA_WHOLE)
         quantise_part(SECOND, 0)
         first_h = sbuf([P, 2, HALF, 4], BF16, f"raw{SECOND}0_0")
         for h in range(2):
             relu(FIRST, h, first_h[:, h])
-        hidden_quantise(FIRST, 0, rows_pool.tile([P, HALF], U32, name="first_codes0", align_bytes=ALIGN, offset=256)[:])
+        hidden_quantise(FIRST, 0, rows_pool.tile([P, HALF], U32, name="first_codes0", align_bytes=ALIGN, offset=2048)[:])
         share_copies(SECOND, 1, 0, PASS, EXTRA_FOURTH)
         quantise_part(SECOND, 1)
         hidden_quantise(FIRST, 1, codes_tile(f"raw{SECOND}1_0"))
@@ -223,9 +224,9 @@ def tile_list_tabmlp_mix_res_kernel(
         relu(SECOND, 1, last.tile([P, HALF, 4], BF16, name="second_h1", align_bytes=ALIGN, offset=0)[:])
         hidden_matmuls(LAST, early_first_bank)
         hidden_quantise(SECOND, 0, last.tile([P, HALF], U32, name="second_codes0", align_bytes=ALIGN, offset=1024)[:])
-        for h in range(2):
-            relu(LAST, h, sbuf([P, HALF, 4], BF16, f"h_grouped{h}")[:])
-        hidden_quantise(LAST, 0, codes_tile(f"w1_codes{LAST}1"))
+        relu(LAST, 0, rows_pool.tile([P, HALF, 4], BF16, name="last_h0", align_bytes=ALIGN, offset=1024)[:])
+        relu(LAST, 1, sbuf([P, HALF, 4], BF16, "last_h1")[:])
+        hidden_quantise(LAST, 0, codes_tile("last_codes0"))
 
         bank_tags = {(0, 0): "out0", (1, 0): "out1", (0, 1): "out2", (1, 1): "out3"}
         sums = {q: psum.tile([P, 2, HALF], F32, name=bank_tags[q]) for q in quarters}
@@ -260,7 +261,7 @@ def tile_list_tabmlp_mix_res_kernel(
             for g in range(2):
                 out_passes(g, 0, step)
         for i, b in enumerate((SECOND, LAST)):
-            tile = rows_pool.tile([P, HALF], U32, name=f"late_codes{i}", align_bytes=ALIGN, offset=4 * HALF * i)
+            tile = rows_pool.tile([P, HALF], U32, name=f"late_codes{i}", align_bytes=ALIGN, offset=1792 + 4 * HALF * i)
             hidden_quantise(b, 1, tile[:])
         out_passes(0, 1, 0)
         for g in range(2):

@@ -41,9 +41,7 @@ def tile_list_tabmlp_mix_res_kernel(
         offsets = keep.tile([P, S // 16], U16, name="offsets")
         table_words = sbuf([P, 2, T], I32, "table_words")
         table_scales = sbuf([P, 2, T // 4], I32, "table_scales")
-        w2_planes = sbuf([P, 2 * (M // 4) + HALF // 4], I32, "w2_planes")
-        w4_planes = w2_planes[:, 0 : 2 * (M // 4)].rearrange("p (a c) -> p a c", a=2)
-        w8_planes = w2_planes[:, 2 * (M // 4) :]
+        w2_planes = sbuf([P, 3, M // 4], I32, "w2_planes")
         w8_codes = sbuf([P, M], I32, "w8_codes")
         w4_codes = sbuf([P, 2, M // 2], I32, "w4_codes")
         quarters = [(g, h) for h in range(2) for g in range(2)]
@@ -51,8 +49,7 @@ def tile_list_tabmlp_mix_res_kernel(
         prev_sb = [sbuf([P, 4, HALF], F32, f"prev_sb{h}") for h in range(2)]
 
         nc.vector.memset(table_scales[:], 0)
-        nc.vector.memset(w8_planes, 0)
-        nc.vector.memset(w4_planes, 0)
+        nc.vector.memset(w2_planes[:], 0)
 
         raws = {}
 
@@ -81,15 +78,13 @@ def tile_list_tabmlp_mix_res_kernel(
         load_w1(FIRST, 1, 0, PASS)
         for a in range(2):
             load_w1(SECOND, a, 0, PASS)
-        w8_rows = w8_scales.bitcast(I32)[0].rearrange("(q r) (m c) -> q m r c", r=4, m=4)
-        for q in range(4):
-            nc.sync.dma_start(w8_planes[32 * q : 32 * q + 16], w8_rows[q])
+        load_scale_rows(w2_planes[:, 0:1], w8_scales.bitcast(I32))
         load_w1(LAST, 0, 0, 256)
         load_w1(LAST, 0, 256, 512)
         load_w1(LAST, 1, 0, 256)
         load_w1(LAST, 1, 256, 384)
         load_w1(LAST, 1, 384, 512)
-        load_scale_rows(w4_planes, w4_scales.bitcast(I32))
+        load_scale_rows(w2_planes[:, 1:3], w4_scales.bitcast(I32))
         nc.sync.dma_start(w4_codes[:], w4_words.bitcast(I32).rearrange("a p c -> p a c"))
         nc.sync.dma_start(w8_codes[:], w8_words[0].rearrange("p n i -> p (n i)").bitcast(I32))
         for h in range(2):
@@ -148,9 +143,9 @@ def tile_list_tabmlp_mix_res_kernel(
                 for t in range(2):
                     quantise(b, a, u, 512 * t, 512 * (t + 1))
 
-        def quantise_half_slices(u, upper):
+        def quantise_piece(u, c0, c1):
             for t in range(2):
-                quantise(LAST, 1, u, 512 * t + 256 * upper, 512 * t + 256 * (upper + 1))
+                quantise(LAST, 1, u, 512 * t + c0, 512 * t + c1)
 
         banks = {}
         in_order = [(a, t) for a in range(2) for t in range(4)]
@@ -197,10 +192,10 @@ def tile_list_tabmlp_mix_res_kernel(
 
         for a in range(2):
             share_copies(FIRST, a, 0, PASS, EXTRA_WHOLE)
-            (quantise_part if a else quantise_slices)(FIRST, a)
+            quantise_slices(FIRST, a)
         hidden_matmuls(FIRST, early_first_bank)
         share_copies(SECOND, 0, 0, PASS, EXTRA_WHOLE)
-        quantise_part(SECOND, 0)
+        quantise_slices(SECOND, 0)
         first_h = sbuf([P, 2, HALF, 4], BF16, f"raw{SECOND}0_0")
         for h in range(2):
             relu(FIRST, h, first_h[:, h])
@@ -211,67 +206,62 @@ def tile_list_tabmlp_mix_res_kernel(
         hidden_matmuls(SECOND, one_stretch)
 
         share_copies(LAST, 0, 0, 256, 0)
-        share_copies(LAST, 0, 256, 512, EXTRA_HALF)
+        share_copies(LAST, 0, 256, 512, 0)
         quantise_part(LAST, 0)
-        relu(SECOND, 0, sbuf([P, HALF, 4], BF16, f"raw{LAST}0_256")[:])
-        share_copies(LAST, 1, 0, 256, EXTRA_HALF)
+        share_copies(LAST, 1, 0, 256, 0)
+        quantise_piece(0, 0, 256)
         share_copies(LAST, 1, 256, 384, 0)
-        quantise_half_slices(0, 0)
         share_copies(LAST, 1, 384, 512, 0)
-        quantise_half_slices(1, 0)
-        quantise_half_slices(0, 1)
-        quantise_half_slices(1, 1)
-        relu(SECOND, 1, last.tile([P, HALF, 4], BF16, name="second_h1", align_bytes=ALIGN, offset=0)[:])
+        quantise_piece(1, 0, 256)
+        quantise_piece(0, 256, 512)
+        quantise_piece(1, 256, 512)
+        relu(SECOND, 0, last.tile([P, HALF, 4], BF16, name="second_h0", align_bytes=ALIGN, offset=0)[:])
+        h_grouped[SECOND, 1] = last.tile([P, HALF, 4], BF16, name="second_h1", align_bytes=ALIGN, offset=1024)[:]
+        nc.vector.tensor_scalar_max(h_grouped[SECOND, 1], banks[SECOND, 1][:].rearrange("p t n -> p n t"), 0.0)
         hidden_matmuls(LAST, early_first_bank)
-        hidden_quantise(SECOND, 0, last.tile([P, HALF], U32, name="second_codes0", align_bytes=ALIGN, offset=1024)[:])
+        hidden_quantise(SECOND, 0, codes_tile("second_codes0"))
         relu(LAST, 0, rows_pool.tile([P, HALF, 4], BF16, name="last_h0", align_bytes=ALIGN, offset=1024)[:])
         relu(LAST, 1, sbuf([P, HALF, 4], BF16, "last_h1")[:])
         hidden_quantise(LAST, 0, codes_tile("last_codes0"))
 
-        bank_tags = {(0, 0): "out0", (1, 0): "out1", (0, 1): "out2", (1, 1): "out3"}
-        sums = {q: psum.tile([P, 2, HALF], F32, name=bank_tags[q]) for q in quarters}
-        block_order = {
-            (0, 0): (FIRST, SECOND, LAST),
-            (1, 0): (FIRST, SECOND, LAST),
-            (0, 1): (FIRST, SECOND, LAST),
-            (1, 1): (SECOND, FIRST, LAST),
-        }
+        bank_tags = ["out0", "out1", "out2", "out3", "hidden10"]
+        sums = [psum.tile([P, i1 - i0, HALF], F32, name=tag) for (g, h, i0, i1), tag in zip(pieces, bank_tags)]
+        block_order = [(FIRST, SECOND, LAST)] * 4 + [(SECOND, FIRST, LAST)]
 
-        def out_passes(g, h, step):
-            b = block_order[g, h][step]
-            for i in range(2):
+        def out_passes(n, step):
+            g, h, i0, i1 = pieces[n]
+            b = block_order[n][step]
+            for i in range(i0, i1):
                 m = 2 * g + i
                 if b == LAST:
                     weights = w8_codes[:, HALF * m : HALF * (m + 1)].bitcast(FP8)
-                    plane = w8_planes[4 * m : P]
                 else:
                     weights = w4_codes[:, b - 1, 64 * m : 64 * (m + 1)].bitcast(FP4)
-                    plane = w4_planes[:, b - 1, 32 * m : 32 * (m + 1)]
                 nc.tensor.matmul_mx(
-                    out=sums[g, h][:, i, :],
+                    out=sums[n][:, i - i0, :],
                     lhsT=weights,
-                    lhsT_scale=plane.bitcast(U8),
+                    lhsT_scale=w2_planes[:, b, 32 * m : 32 * (m + 1)].bitcast(U8),
                     rhs=h_codes[b, h].bitcast(FP8),
                     rhs_scale=h_scales[b][:, HALF * h : HALF * (h + 1)],
-                    start=(step, i) == (0, 0),
-                    stop=(step, i) == (2, 1),
+                    start=(step, i) == (0, i0),
+                    stop=(step, i) == (2, i1 - 1),
                 )
 
         for step in range(2):
-            for g in range(2):
-                out_passes(g, 0, step)
+            for n in range(3):
+                out_passes(n, step)
         for i, b in enumerate((SECOND, LAST)):
             tile = rows_pool.tile([P, HALF], U32, name=f"late_codes{i}", align_bytes=ALIGN, offset=1792 + 4 * HALF * i)
             hidden_quantise(b, 1, tile[:])
-        out_passes(0, 1, 0)
-        for g in range(2):
-            out_passes(g, 0, 2)
-        out_passes(0, 1, 1)
-        out_passes(0, 1, 2)
+        out_passes(3, 0)
+        for n in range(3):
+            out_passes(n, 2)
+        out_passes(3, 1)
+        out_passes(3, 2)
         for step in range(3):
-            out_passes(1, 1, step)
+            out_passes(4, step)
 
-        for g, h, i0, i1 in pieces:
+        for n, (g, h, i0, i1) in enumerate(pieces):
             result = sbuf([P, i1 - i0, HALF], F32, f"result{g}{h}{i0}")
-            nc.vector.tensor_add(result[:], sums[g, h][:, i0:i1], prev_sb[h][:, 2 * g + i0 : 2 * g + i1])
+            nc.vector.tensor_add(result[:], sums[n][:], prev_sb[h][:, 2 * g + i0 : 2 * g + i1])
             nc.sync.dma_start(quarter(out, g, h)[:, i0:i1], result[:])

@@ -11,7 +11,7 @@ HALF = 128
 WORD_BYTES = 512 * T
 ALIGN = 256
 
-FIRST, SECOND, LAST = 1, 2, 0
+FIRST, SECOND, LAST = 1, 0, 2
 EXTRA_WHOLE, EXTRA_HALF, EXTRA_FOURTH = 32, 16, 16
 
 F32 = mybir.dt.float32
@@ -32,7 +32,6 @@ def tile_list_tabmlp_mix_res_kernel(
     with ExitStack() as ctx:
         keep = ctx.enter_context(tc.tile_pool(name="keep", bufs=1))
         last = ctx.enter_context(tc.tile_pool(name="last", bufs=1))
-        rows_pool = ctx.enter_context(tc.tile_pool(name="rows", bufs=1))
         psum = ctx.enter_context(tc.psum_pool(name="psum", bufs=1))
 
         def sbuf(shape, dtype, name):
@@ -49,7 +48,8 @@ def tile_list_tabmlp_mix_res_kernel(
         prev_sb = [sbuf([P, 4, HALF], F32, f"prev_sb{h}") for h in range(2)]
 
         nc.vector.memset(table_scales[:], 0)
-        nc.vector.memset(w2_planes[:], 0)
+        nc.vector.memset(w2_planes[:, 1:3], 0)
+        nc.vector.memset(w2_planes[:, 0:1], 0)
 
         raws = {}
 
@@ -78,7 +78,6 @@ def tile_list_tabmlp_mix_res_kernel(
         load_w1(FIRST, 1, 0, PASS)
         for a in range(2):
             load_w1(SECOND, a, 0, PASS)
-        load_scale_rows(w2_planes[:, 0:1], w8_scales.bitcast(I32))
         load_w1(LAST, 0, 0, 256)
         load_w1(LAST, 0, 256, 512)
         load_w1(LAST, 1, 0, 256)
@@ -87,6 +86,7 @@ def tile_list_tabmlp_mix_res_kernel(
         load_scale_rows(w2_planes[:, 1:3], w4_scales.bitcast(I32))
         nc.sync.dma_start(w4_codes[:], w4_words.bitcast(I32).rearrange("a p c -> p a c"))
         nc.sync.dma_start(w8_codes[:], w8_words[0].rearrange("p n i -> p (n i)").bitcast(I32))
+        load_scale_rows(w2_planes[:, 0:1], w8_scales.bitcast(I32))
         for h in range(2):
             nc.sync.dma_start(prev_sb[h][:], prev[:, HALF * h : HALF * (h + 1)].rearrange("(m p) j -> p m j", p=P))
 
@@ -105,10 +105,7 @@ def tile_list_tabmlp_mix_res_kernel(
         for b in range(3):
             for a in range(2):
                 for u in range(2):
-                    if (b, a, u) == (SECOND, 0, 1):
-                        grouped[b, a, u] = rows_pool.tile([P, 1024], BF16, name="third", align_bytes=ALIGN, offset=2048)
-                    else:
-                        grouped[b, a, u] = sbuf([P, 1024], BF16, f"grouped{b}{a}{u}")
+                    grouped[b, a, u] = sbuf([P, 1024], BF16, f"grouped{b}{a}{u}")
                 codes[b, a] = sbuf([P, PASS], U32, f"w1_codes{b}{a}")
                 scales[b, a] = sbuf([P, PASS], U8, f"w1_scales{b}{a}")
 
@@ -192,14 +189,14 @@ def tile_list_tabmlp_mix_res_kernel(
 
         for a in range(2):
             share_copies(FIRST, a, 0, PASS, EXTRA_WHOLE)
-            quantise_slices(FIRST, a)
+            (quantise_part if a else quantise_slices)(FIRST, a)
         hidden_matmuls(FIRST, early_first_bank)
         share_copies(SECOND, 0, 0, PASS, EXTRA_WHOLE)
-        quantise_slices(SECOND, 0)
+        quantise_part(SECOND, 0)
         first_h = sbuf([P, 2, HALF, 4], BF16, f"raw{SECOND}0_0")
         for h in range(2):
             relu(FIRST, h, first_h[:, h])
-        hidden_quantise(FIRST, 0, rows_pool.tile([P, HALF], U32, name="first_codes0", align_bytes=ALIGN, offset=2048)[:])
+        hidden_quantise(FIRST, 0, codes_tile(f"grouped{SECOND}01"))
         share_copies(SECOND, 1, 0, PASS, EXTRA_FOURTH)
         quantise_part(SECOND, 1)
         hidden_quantise(FIRST, 1, codes_tile(f"raw{SECOND}1_0"))
@@ -220,20 +217,21 @@ def tile_list_tabmlp_mix_res_kernel(
         nc.vector.tensor_scalar_max(h_grouped[SECOND, 1], banks[SECOND, 1][:].rearrange("p t n -> p n t"), 0.0)
         hidden_matmuls(LAST, early_first_bank)
         hidden_quantise(SECOND, 0, codes_tile("second_codes0"))
-        relu(LAST, 0, rows_pool.tile([P, HALF, 4], BF16, name="last_h0", align_bytes=ALIGN, offset=1024)[:])
-        relu(LAST, 1, sbuf([P, HALF, 4], BF16, "last_h1")[:])
-        hidden_quantise(LAST, 0, codes_tile("last_codes0"))
+        hidden_quantise(SECOND, 1, codes_tile("second_codes1"))
+        for h in range(2):
+            relu(LAST, h, sbuf([P, HALF, 4], BF16, f"last_h{h}")[:])
+            hidden_quantise(LAST, h, codes_tile(f"last_codes{h}"))
 
         bank_tags = ["out0", "out1", "out2", "out3", "hidden10"]
         sums = [psum.tile([P, i1 - i0, HALF], F32, name=tag) for (g, h, i0, i1), tag in zip(pieces, bank_tags)]
-        block_order = [(FIRST, SECOND, LAST)] * 4 + [(SECOND, FIRST, LAST)]
+        block_order = (FIRST, SECOND, LAST)
 
         def out_passes(n, step):
             g, h, i0, i1 = pieces[n]
-            b = block_order[n][step]
+            b = block_order[step]
             for i in range(i0, i1):
                 m = 2 * g + i
-                if b == LAST:
+                if b == 0:
                     weights = w8_codes[:, HALF * m : HALF * (m + 1)].bitcast(FP8)
                 else:
                     weights = w4_codes[:, b - 1, 64 * m : 64 * (m + 1)].bitcast(FP4)
@@ -247,19 +245,12 @@ def tile_list_tabmlp_mix_res_kernel(
                     stop=(step, i) == (2, i1 - 1),
                 )
 
-        for step in range(2):
-            for n in range(3):
-                out_passes(n, step)
-        for i, b in enumerate((SECOND, LAST)):
-            tile = rows_pool.tile([P, HALF], U32, name=f"late_codes{i}", align_bytes=ALIGN, offset=1792 + 4 * HALF * i)
-            hidden_quantise(b, 1, tile[:])
-        out_passes(3, 0)
-        for n in range(3):
-            out_passes(n, 2)
-        out_passes(3, 1)
-        out_passes(3, 2)
-        for step in range(3):
-            out_passes(4, step)
+        for n in range(5):
+            out_passes(n, 0)
+        for group in ((0, 1), (2,), (3,), (4,)):
+            for step in (1, 2):
+                for n in group:
+                    out_passes(n, step)
 
         for n, (g, h, i0, i1) in enumerate(pieces):
             result = sbuf([P, i1 - i0, HALF], F32, f"result{g}{h}{i0}")

@@ -62,9 +62,9 @@ def tile_list_tabmlp_mix_res_kernel(
             nc.sync.dma_start(raw[:], rows.rearrange("(p j) c -> p j c", j=4))
             raws[b, a, c0] = raw
 
-        def load_scale_rows(planes, rows):
+        def load_scale_rows(planes, rows, which=range(4)):
             by_r = rows.rearrange("a (q r) c -> r q a c", r=4)
-            for r in range(4):
+            for r in which:
                 nc.sync.dma_start(planes[r:P:32], by_r[r])
 
         def quarter(dram, g, h):
@@ -78,6 +78,7 @@ def tile_list_tabmlp_mix_res_kernel(
         load_w1(FIRST, 1, 0, PASS)
         for a in range(2):
             load_w1(SECOND, a, 0, PASS)
+        load_scale_rows(w2_planes[:, 0:1], w8_scales.bitcast(I32), range(1))
         load_w1(LAST, 0, 0, 256)
         load_w1(LAST, 0, 256, 512)
         load_w1(LAST, 1, 0, 256)
@@ -86,7 +87,7 @@ def tile_list_tabmlp_mix_res_kernel(
         load_scale_rows(w2_planes[:, 1:3], w4_scales.bitcast(I32))
         nc.sync.dma_start(w4_codes[:], w4_words.bitcast(I32).rearrange("a p c -> p a c"))
         nc.sync.dma_start(w8_codes[:], w8_words[0].rearrange("p n i -> p (n i)").bitcast(I32))
-        load_scale_rows(w2_planes[:, 0:1], w8_scales.bitcast(I32))
+        load_scale_rows(w2_planes[:, 0:1], w8_scales.bitcast(I32), range(1, 4))
         for h in range(2):
             nc.sync.dma_start(prev_sb[h][:], prev[:, HALF * h : HALF * (h + 1)].rearrange("(m p) j -> p m j", p=P))
 
@@ -135,11 +136,6 @@ def tile_list_tabmlp_mix_res_kernel(
             for u in range(2):
                 quantise(b, a, u, 0, 1024)
 
-        def quantise_slices(b, a):
-            for u in range(2):
-                for t in range(2):
-                    quantise(b, a, u, 512 * t, 512 * (t + 1))
-
         def quantise_piece(u, c0, c1):
             for t in range(2):
                 quantise(LAST, 1, u, 512 * t + c0, 512 * t + c1)
@@ -172,24 +168,28 @@ def tile_list_tabmlp_mix_res_kernel(
         for b in range(3):
             h_scales[b] = sbuf([P, S], U8, f"h_scales{b}")
 
-        def relu(b, h, dst):
+        def relu(b, h, dst, cuts=1):
             h_grouped[b, h] = dst
-            nc.scalar.activation(dst, banks[b, h][:].rearrange("p t n -> p n t"), RELU)
+            by_token = banks[b, h][:].rearrange("p t n -> p n t")
+            for n0 in range(0, HALF, HALF // cuts):
+                nc.scalar.activation(dst[:, n0 : n0 + HALF // cuts], by_token[:, n0 : n0 + HALF // cuts], RELU)
 
         def codes_tile(tag):
             return sbuf([P, HALF], U32, tag)[:]
 
-        def hidden_quantise(b, h, dst):
+        def hidden_quantise(b, h, dst, cuts=1):
             h_codes[b, h] = dst
-            nc.vector.quantize_mx(
-                out=dst.bitcast(FP8),
-                scales=h_scales[b][:, HALF * h : HALF * (h + 1)],
-                in_=h_grouped[b, h].rearrange("p n t -> p (n t)"),
-            )
+            for n0 in range(0, HALF, HALF // cuts):
+                n1 = n0 + HALF // cuts
+                nc.vector.quantize_mx(
+                    out=dst[:, n0:n1].bitcast(FP8),
+                    scales=h_scales[b][:, HALF * h + n0 : HALF * h + n1],
+                    in_=h_grouped[b, h][:, n0:n1].rearrange("p n t -> p (n t)"),
+                )
 
         for a in range(2):
             share_copies(FIRST, a, 0, PASS, EXTRA_WHOLE)
-            (quantise_part if a else quantise_slices)(FIRST, a)
+            quantise_part(FIRST, a)
         hidden_matmuls(FIRST, early_first_bank)
         share_copies(SECOND, 0, 0, PASS, EXTRA_WHOLE)
         quantise_part(SECOND, 0)
@@ -219,8 +219,8 @@ def tile_list_tabmlp_mix_res_kernel(
         hidden_quantise(SECOND, 0, codes_tile("second_codes0"))
         hidden_quantise(SECOND, 1, codes_tile("second_codes1"))
         for h in range(2):
-            relu(LAST, h, sbuf([P, HALF, 4], BF16, f"last_h{h}")[:])
-            hidden_quantise(LAST, h, codes_tile(f"last_codes{h}"))
+            relu(LAST, h, sbuf([P, HALF, 4], BF16, f"last_h{h}")[:], 2)
+            hidden_quantise(LAST, h, codes_tile(f"last_codes{h}"), 2)
 
         bank_tags = ["out0", "out1", "out2", "out3", "hidden10"]
         sums = [psum.tile([P, i1 - i0, HALF], F32, name=tag) for (g, h, i0, i1), tag in zip(pieces, bank_tags)]

from contextlib import ExitStack

import concourse.mybir as mybir

FLOPS = 1207959552

P = 128
PASS = 512
M, T, S = 512, 512, 256
HALF = 128
WORD_BYTES = 512 * T
ALIGN = 256

FIRST, SECOND, LAST = 1, 0, 2
EXTRA_WHOLE, EXTRA_HALF, EXTRA_FOURTH = 32, 16, 16

F32 = mybir.dt.float32
BF16 = mybir.dt.bfloat16
I32 = mybir.dt.int32
U32 = mybir.dt.uint32
U16 = mybir.dt.uint16
U8 = mybir.dt.uint8
FP8 = mybir.dt.float8_e4m3fn_x4
FP4 = mybir.dt.float4_e2m1fn_x4
RELU = mybir.ActivationFunctionType.Relu


def tile_list_tabmlp_mix_res_kernel(
    tc, tab, w1, w8_words, w8_scales, w4_words, w4_scales, prev, offs, out
):
    nc = tc.nc
    with ExitStack() as ctx:
        keep = ctx.enter_context(tc.tile_pool(name="keep", bufs=1))
        last = ctx.enter_context(tc.tile_pool(name="last", bufs=1))
        psum = ctx.enter_context(tc.psum_pool(name="psum", bufs=1))

        def sbuf(shape, dtype, name):
            return keep.tile(shape, dtype, name=name, align_bytes=ALIGN)

        offsets = keep.tile([P, S // 16], U16, name="offsets")
        table_words = sbuf([P, 2, T], I32, "table_words")
        table_scales = sbuf([P, 2, T // 4], I32, "table_scales")
        w2_planes = sbuf([P, 3, M // 4], I32, "w2_planes")
        w8_codes = sbuf([P, M], I32, "w8_codes")
        w4_codes = sbuf([P, 2, M // 2], I32, "w4_codes")
        quarters = [(g, h) for h in range(2) for g in range(2)]
        pieces = [(0, 0, 0, 1), (0, 0, 1, 2)] + [(g, h, 0, 2) for g, h in quarters[1:]]
        prev_sb = [sbuf([P, 4, HALF], F32, f"prev_sb{h}") for h in range(2)]

        nc.vector.memset(table_scales[:], 0)
        nc.vector.memset(w2_planes[:, 1:3], 0)
        nc.vector.memset(w2_planes[:, 0:1], 0)

        raws = {}

        def load_w1(b, a, c0, c1):
            if (b, a, c1) == (LAST, 1, PASS):
                raw = last.tile([P, 4, c1 - c0], F32, name="last_raw", align_bytes=ALIGN, offset=0)
            else:
                raw = sbuf([P, 4, c1 - c0], F32, f"raw{b}{a}_{c0}")
            rows = w1[PASS * a : PASS * (a + 1), PASS * b + c0 : PASS * b + c1]
            nc.sync.dma_start(raw[:], rows.rearrange("(p j) c -> p j c", j=4))
            raws[b, a, c0] = raw

        def load_scale_rows(planes, rows, which=range(4)):
            by_r = rows.rearrange("a (q r) c -> r q a c", r=4)
            for r in which:
                nc.sync.dma_start(planes[r:P:32], by_r[r])

        def quarter(dram, g, h):
            return dram[256 * g : 256 * (g + 1), HALF * h : HALF * (h + 1)].rearrange("(m p) j -> p m j", p=P)

        tab_i32 = tab.bitcast(I32)
        nc.sync.dma_start(table_words[:], tab_i32[:, 0 : WORD_BYTES // 4].rearrange("a (p c) -> p a c", p=P))
        nc.sync.dma_start(offsets[:], offs)
        load_w1(FIRST, 0, 0, PASS)
        load_scale_rows(table_scales[:], tab_i32[:, WORD_BYTES // 4 :].rearrange("a (q c) -> a q c", q=16))
        load_w1(FIRST, 1, 0, PASS)
        for a in range(2):
            load_w1(SECOND, a, 0, PASS)
        load_scale_rows(w2_planes[:, 0:1], w8_scales.bitcast(I32), range(1))
        load_w1(LAST, 0, 0, 256)
        load_w1(LAST, 0, 256, 512)
        load_w1(LAST, 1, 0, 256)
        load_w1(LAST, 1, 256, 384)
        load_w1(LAST, 1, 384, 512)
        load_scale_rows(w2_planes[:, 1:3], w4_scales.bitcast(I32))
        nc.sync.dma_start(w4_codes[:], w4_words.bitcast(I32).rearrange("a p c -> p a c"))
        nc.sync.dma_start(w8_codes[:], w8_words[0].rearrange("p n i -> p (n i)").bitcast(I32))
        load_scale_rows(w2_planes[:, 0:1], w8_scales.bitcast(I32), range(1, 4))
        for h in range(2):
            nc.sync.dma_start(prev_sb[h][:], prev[:, HALF * h : HALF * (h + 1)].rearrange("(m p) j -> p m j", p=P))

        picked_words = []
        for a in range(2):
            words = sbuf([P, S], U32, f"picked_words{a}")
            nc.vector.tensor_copy(words[:], table_words[:, a, :].bitcast(U32).indirect(offsets[:]))
            picked_words.append(words)
        picked_scales = []
        for a in range(2):
            scale_bytes = sbuf([P, S], U8, f"picked_scales{a}")
            nc.vector.tensor_copy(scale_bytes[:], table_scales[:, a, :].bitcast(U8).indirect(offsets[:]))
            picked_scales.append(scale_bytes)

        grouped, codes, scales = {}, {}, {}
        for b in range(3):
            for a in range(2):
                for u in range(2):
                    grouped[b, a, u] = sbuf([P, 1024], BF16, f"grouped{b}{a}{u}")
                codes[b, a] = sbuf([P, PASS], U32, f"w1_codes{b}{a}")
                scales[b, a] = sbuf([P, PASS], U8, f"w1_scales{b}{a}")

        def interleave(engine, b, a, c0, u, m0, m1):
            dst = grouped[b, a, u][:].rearrange("p (t m j) -> p m j t", t=2, j=4)[:, m0:m1]
            src = raws[b, a, c0][:].rearrange("p j (m t) -> p m j t", t=4)
            src = src[:, m0 - c0 // 4 : m1 - c0 // 4, :, 2 * u : 2 * u + 2]
            if engine is nc.scalar:
                nc.scalar.copy(dst, src)
            else:
                nc.vector.tensor_copy(dst, src)

        def share_copies(b, a, c0, c1, extra):
            m0, m1 = c0 // 4, c1 // 4
            interleave(nc.scalar, b, a, c0, 1, m0 + extra, m1)
            interleave(nc.vector, b, a, c0, 0, m0, m1)
            if extra:
                interleave(nc.vector, b, a, c0, 1, m0, m0 + extra)

        def quantise(b, a, u, i0, i1):
            cols = slice(256 * u + i0 // 4, 256 * u + i1 // 4)
            nc.vector.quantize_mx(
                out=codes[b, a][:, cols].bitcast(FP8), scales=scales[b, a][:, cols], in_=grouped[b, a, u][:, i0:i1]
            )

        def quantise_part(b, a):
            for u in range(2):
                quantise(b, a, u, 0, 1024)

        def quantise_piece(u, c0, c1):
            for t in range(2):
                quantise(LAST, 1, u, 512 * t + c0, 512 * t + c1)

        banks = {}
        in_order = [(a, t) for a in range(2) for t in range(4)]

        def hidden_matmuls(b, passes):
            for h in range(2):
                banks[b, h] = psum.tile([P, 4, HALF], F32, name=f"hidden{int(b == SECOND)}{h}")
            for a, t, h in passes:
                cols = slice(HALF * t, HALF * (t + 1))
                toks = slice(HALF * h, HALF * (h + 1))
                of_bank = [step for step in passes if step[2] == h]
                nc.tensor.matmul_mx(
                    out=banks[b, h][:, t, :],
                    lhsT=codes[b, a][:, cols].bitcast(FP8),
                    lhsT_scale=scales[b, a][:, cols],
                    rhs=picked_words[a][:, toks].bitcast(FP8),
                    rhs_scale=picked_scales[a][:, toks],
                    start=(a, t, h) == of_bank[0],
                    stop=(a, t, h) == of_bank[-1],
                )

        early_first_bank = [(0, t, h) for t in range(4) for h in range(2)]
        early_first_bank.extend((1, t, h) for h in range(2) for t in range(4))
        one_stretch = [(a, t, h) for h in range(2) for a, t in in_order[4:6] + in_order[0:4] + in_order[6:8]]

        h_grouped, h_codes, h_scales = {}, {}, {}
        for b in range(3):
            h_scales[b] = sbuf([P, S], U8, f"h_scales{b}")

        def relu(b, h, dst, cuts=1):
            h_grouped[b, h] = dst
            by_token = banks[b, h][:].rearrange("p t n -> p n t")
            for n0 in range(0, HALF, HALF // cuts):
                nc.scalar.activation(dst[:, n0 : n0 + HALF // cuts], by_token[:, n0 : n0 + HALF // cuts], RELU)

        def codes_tile(tag):
            return sbuf([P, HALF], U32, tag)[:]

        def hidden_quantise(b, h, dst, cuts=1):
            h_codes[b, h] = dst
            for n0 in range(0, HALF, HALF // cuts):
                n1 = n0 + HALF // cuts
                nc.vector.quantize_mx(
                    out=dst[:, n0:n1].bitcast(FP8),
                    scales=h_scales[b][:, HALF * h + n0 : HALF * h + n1],
                    in_=h_grouped[b, h][:, n0:n1].rearrange("p n t -> p (n t)"),
                )

        for a in range(2):
            share_copies(FIRST, a, 0, PASS, EXTRA_WHOLE)
            quantise_part(FIRST, a)
        hidden_matmuls(FIRST, early_first_bank)
        share_copies(SECOND, 0, 0, PASS, EXTRA_WHOLE)
        quantise_part(SECOND, 0)
        first_h = sbuf([P, 2, HALF, 4], BF16, f"raw{SECOND}0_0")
        for h in range(2):
            relu(FIRST, h, first_h[:, h])
        hidden_quantise(FIRST, 0, codes_tile(f"grouped{SECOND}01"))
        share_copies(SECOND, 1, 0, PASS, EXTRA_FOURTH)
        quantise_part(SECOND, 1)
        hidden_quantise(FIRST, 1, codes_tile(f"raw{SECOND}1_0"))
        hidden_matmuls(SECOND, one_stretch)

        share_copies(LAST, 0, 0, 256, 0)
        share_copies(LAST, 0, 256, 512, 0)
        quantise_part(LAST, 0)
        share_copies(LAST, 1, 0, 256, 0)
        quantise_piece(0, 0, 256)
        share_copies(LAST, 1, 256, 384, 0)
        share_copies(LAST, 1, 384, 512, 0)
        quantise_piece(1, 0, 256)
        quantise_piece(0, 256, 512)
        quantise_piece(1, 256, 512)
        relu(SECOND, 0, last.tile([P, HALF, 4], BF16, name="second_h0", align_bytes=ALIGN, offset=0)[:])
        h_grouped[SECOND, 1] = last.tile([P, HALF, 4], BF16, name="second_h1", align_bytes=ALIGN, offset=1024)[:]
        nc.vector.tensor_scalar_max(h_grouped[SECOND, 1], banks[SECOND, 1][:].rearrange("p t n -> p n t"), 0.0)
        hidden_matmuls(LAST, early_first_bank)
        hidden_quantise(SECOND, 0, codes_tile("second_codes0"))
        hidden_quantise(SECOND, 1, codes_tile("second_codes1"))
        for h in range(2):
            relu(LAST, h, sbuf([P, HALF, 4], BF16, f"last_h{h}")[:], 2)
            hidden_quantise(LAST, h, codes_tile(f"last_codes{h}"), 2)

        bank_tags = ["out0", "out1", "out2", "out3", "hidden10"]
        sums = [psum.tile([P, i1 - i0, HALF], F32, name=tag) for (g, h, i0, i1), tag in zip(pieces, bank_tags)]
        block_order = (FIRST, SECOND, LAST)

        def out_passes(n, step):
            g, h, i0, i1 = pieces[n]
            b = block_order[step]
            for i in range(i0, i1):
                m = 2 * g + i
                if b == 0:
                    weights = w8_codes[:, HALF * m : HALF * (m + 1)].bitcast(FP8)
                else:
                    weights = w4_codes[:, b - 1, 64 * m : 64 * (m + 1)].bitcast(FP4)
                nc.tensor.matmul_mx(
                    out=sums[n][:, i - i0, :],
                    lhsT=weights,
                    lhsT_scale=w2_planes[:, b, 32 * m : 32 * (m + 1)].bitcast(U8),
                    rhs=h_codes[b, h].bitcast(FP8),
                    rhs_scale=h_scales[b][:, HALF * h : HALF * (h + 1)],
                    start=(step, i) == (0, i0),
                    stop=(step, i) == (2, i1 - 1),
                )

        for n in range(5):
            out_passes(n, 0)
        for group in ((0, 1), (2,), (3,), (4,)):
            for step in (1, 2):
                for n in group:
                    out_passes(n, step)

        for n, (g, h, i0, i1) in enumerate(pieces):
            result = sbuf([P, i1 - i0, HALF], F32, f"result{g}{h}{i0}")
            nc.vector.tensor_add(result[:], sums[n][:], prev_sb[h][:, 2 * g + i0 : 2 * g + i1])
            nc.sync.dma_start(quarter(out, g, h)[:, i0:i1], result[:])
